import numpy as np, ml_dtypes
CORES = [23,119,17,113]
N = 4
BF = ml_dtypes.bfloat16
W, A, S, CAP, RO = 4096, 1024, 4, 128, 5
P, BL = A // S, W // CAP
WT = 2 * np.arange(16) + 1
def counts(rng, fat):
    return np.where(fat, rng.integers(9, 17, fat.shape), rng.integers(0, 9, fat.shape))
def cols(rng, n, top):
    on = np.argsort(rng.random((N, 8, 16, W)), axis=2) < n[:, :, None, :]
    return np.where(on, 1 + (top * rng.random((N, 8, 16, W))).astype(np.int64), 0)
def lines(rng, fat, share):
    o = np.argsort(np.where(fat, 0.0, 1.0) + 0.5 * rng.random((N, 8, W)), axis=-1); nf = np.add.reduce(fat.astype(np.int64), axis=-1)[:, :, None, None]
    v = rng.random((N, 8, 16, A))
    k = np.where(rng.random((N, 8, 16, A)) < share, (v * nf).astype(np.int64), nf + (v * (W - nf)).astype(np.int64))
    return np.take_along_axis(o, k.reshape(N, 8, 16 * A), 2).reshape(N, 8, 16, A)
def hop(e, u):
    return (((e * u) >> 5) + e) & (W - 1)
def first(X):
    u = np.add.reduce(X * WT.reshape(1, 1, 16, 1), axis=2) & (W - 1); h = hop(np.arange(W).reshape(1, 1, W), u)
    y = np.take_along_axis(X, h[:, :, None, :], 3)
    return np.add.reduce(np.sign(y - X), axis=2), np.add.reduce((X > 0).astype(np.int64), axis=2)
def top16(s):
    v = np.full(16, 255); d = (65280 - s) & (W - 1)
    for w in range(15, -1, -1):
        c = min(254, d // (2 * w + 1)); v[w] -= c; d -= c * (2 * w + 1)
    return v
def pack(X, E, M):
    return {"xt": X.reshape(N, 128, W).astype(np.float32).astype(BF), "led": E.reshape(N, 128, A).astype(np.int32), "mk": M.reshape(N, 128, A).astype(np.float32).astype(BF)}
def setup_inputs(rng):
    fat = rng.random((N, 8, W)) < rng.choice(np.array([0.3, 0.5, 0.7]), (N, 8, 1))
    X = cols(rng, counts(rng, fat), 255)
    share = rng.choice(np.array([0.01, 0.05, 0.15, 0.6]), (N, 8, 1, A)) * rng.choice(np.array([0.2, 1.0, 1.5]), (N, 8, 1, 1))
    return pack(X, lines(rng, fat, share), rng.integers(0, 2, (N, 8, 16, A)))
def setup_inputs_spread(rng):
    fat = rng.random((N, 8, W)) < rng.choice(np.array([0.2, 0.5, 0.8]), (N, 8, 1))
    top = np.minimum(np.exp2(8 * rng.random((N, 8, 1, W))).astype(np.int64), 255)
    X = cols(rng, counts(rng, fat), top)
    E = lines(rng, fat, rng.choice(np.array([0.01, 0.05, 0.2, 0.7]), (N, 8, 1, A)))
    low = (W * rng.random((N, 8, 16, A)) ** 4).astype(np.int64); E = np.where(rng.random((N, 8, 1, A)) < 0.25, low, E)
    return pack(X, E, (rng.random((N, 8, 16, A)) < rng.random((N, 8, 1, A))).astype(np.int64))
def setup_inputs_ends(rng):
    kind = rng.integers(0, 3, (N, 8, 1, W))
    X = np.where(kind == 0, 0, np.where(kind == 1, 255, 255 * rng.integers(0, 2, (N, 8, 16, W))))
    X[..., 1] = 1; X[..., hop(1, 256)] = 255
    X[..., 2] = 255; X[..., hop(2, 65280 & (W - 1))] = 0
    X[..., W - 2] = 254; X[..., hop(W - 2, 65024 & (W - 1))] = 255
    X[..., W - 1] = top16(W - 1); X[..., hop(W - 1, W - 1)] = 0
    sh = (N, 8, 16, A)
    other = np.where(rng.random(sh) < 0.5, rng.choice(np.array([1, 2, W - 2]), sh), rng.integers(0, W, sh))
    E = np.where(rng.random(sh) < 0.7, (W - 1) * rng.integers(0, 2, sh), other)
    M = (rng.random(sh) < rng.choice(np.array([0.0, 0.5, 1.0]), (N, 8, 1, A))).astype(np.int64)
    i = np.arange(P) * S; q = N - 1
    for r in (0, q):
        for g in range(8):
            k = 2 * rng.integers(0, 8, P); E[r, g, k, i] = W - 1; M[r, g, k, i] = 1
    E[1, 0, :, 0::S] = 0; M[1, 0, :, 0::S] = 0
    E[q, 0, :, 0] = 0; M[q, 0, :, 0] = 0
    a, b, c, d = int(i[CAP - 1]), int(i[P - 1]), int(i[P - 2]), int(i[3])
    E[q, 7, :, a] = W - 1; M[q, 7, :, a] = 1
    E[q, 7, :, b] = 0; M[q, 7, :, b] = 0; E[q, 7, 14:, b] = W - 1; M[q, 7, 14:, b] = 1
    E[q, 7, :, c] = 0; M[q, 7, :, c] = 0; E[q, 7, 14, c] = W - 2; M[q, 7, 14, c] = 1; E[q, 7, 15, c] = 1
    E[:, 7, 0::2, d] = 2; M[:, 7, 0::2, d] = 1; E[:, 7, 1::2, d] = W - 1; M[:, 7, 1::2, d] = 0
    return pack(X, E, M)
def setup_inputs_corners(rng):
    fat = rng.random((N, 8, W)) < 0.5; X = cols(rng, counts(rng, fat), 255)
    E = lines(rng, fat, 0.1); M = rng.integers(0, 2, (N, 8, 16, A)); g, n = first(X)
    room = (0, 1, CAP - 1, CAP, CAP + 1, P, CAP, P - 1); even = np.arange(16)[:, None] % 2 == 0
    for q in range(N):
        for b in range(8):
            gg = g[q, b]; hot = np.flatnonzero((n[q, b] >= 9) & (gg != 0)); thin = np.flatnonzero(n[q, b] <= 8)
            c = int(rng.choice(np.array(room)))
            if q == 0: c = room[b]
            if q == N - 1: c = room[(b + 4) % 8]
            o = np.concatenate([np.array([P - 1]), rng.permutation(P - 1)]); yes = o[:c]; z = np.zeros((1, P), bool); z[0, o[c:]] = True
            e = np.where(rng.random((16, P)) < 0.2, (W - 1) * rng.integers(0, 2, (16, P)), rng.integers(0, W, (16, P)))
            m = (rng.random((16, P)) < rng.choice(np.array([0.0, 0.5, 1.0]), (1, P))).astype(np.int64)
            ge = gg[e]; m = np.where(even & z & (ge != 0), (ge > 0).astype(np.int64), m)
            e = np.where(~even & z, rng.choice(thin, (16, P)), e)
            k = 2 * rng.integers(0, 8, c); hh = rng.choice(hot, c); e[k, yes] = hh; m[k, yes] = (gg[hh] < 0).astype(np.int64)
            E[q, b, :, 0::S] = e; M[q, b, :, 0::S] = m
    return pack(X, E, M)
def setup_inputs_ties(rng):
    fat = rng.random((N, 8, W)) < 0.5
    n = np.where(fat, np.where(rng.random((N, 8, W)) < 0.8, 9, 16), 8); X = cols(rng, n, rng.choice(np.array([1, 2, 3]), (N, 8, 1, W)))
    E = lines(rng, fat, rng.choice(np.array([0.02, 0.2, 0.5]), (N, 8, 1, A)))
    E = np.take_along_axis(E, rng.integers(0, 3, (N, 8, 16, A)), 2)
    return pack(X, E, (rng.random((N, 8, 16, A)) < rng.choice(np.array([0.1, 0.5, 0.9]), (N, 8, 1, A))).astype(np.int64))
def setup_inputs_deep(rng):
    fat = rng.random((N, 8, W)) < 0.5; X = cols(rng, counts(rng, fat), 255)
    X[..., 0] = 0
    X[..., 3] = 253; X[..., hop(3, 64768 & (W - 1))] = 255
    X[..., 5] = 252; X[..., hop(5, 64512 & (W - 1))] = 255
    X[..., 7] = 255; X[..., hop(7, 65280 & (W - 1))] = 255; X[..., hop(7, 62976 & (W - 1))] = 255
    X[..., 11] = W >> 8
    X[..., W - 3] = top16(W - 21); X[..., hop(W - 3, W - 21)] = 0; X[..., hop(W - 3, W - 21) + 1] = 255
    X[..., 1001] = 255; X[..., 0, 1001] = 254; X[..., hop(1001, 65279 & (W - 1))] = 0
    X[..., 13] = 0; X[..., 7:, 13] = 255; X[..., hop(13, 52785 & (W - 1))] = 0
    X[..., 17] = 0; X[..., :9, 17] = 255; X[..., hop(17, 20655 & (W - 1))] = 0
    E = lines(rng, fat, 0.1); M = rng.integers(0, 2, (N, 8, 16, A)); s, n = first(X)
    h = hop(np.arange(W).reshape(1, 1, W), np.add.reduce(X * WT.reshape(1, 1, 16, 1), axis=2) & (W - 1))
    kind = np.argsort(rng.random((N, 8, P)), axis=-1) % 7
    for q in range(N):
        for b in range(8):
            if b in (1, 6):
                far = np.arange(W) >= (W >> 2); nn = n[q, b]; hh = h[q, b]
                thin = np.flatnonzero((nn <= 8) & far); hot = np.flatnonzero((nn >= 9) & (s[q, b] < 0) & (nn[hh] <= 8) & far[hh])
                E[q, b] = rng.choice(thin, (16, A))
                c = int(rng.integers(CAP >> 3, (CAP >> 2) + 1)); i = S * rng.permutation(P)[:c]; k = 2 * rng.integers(0, 8, c)
                E[q, b, k, i] = rng.choice(hot, c); M[q, b, k, i] = 1
                continue
            for v in range(1, 7):
                i = S * np.flatnonzero(kind[q, b] == v); k = 2 * rng.integers(0, 8, len(i))
                E[q, b, :, i] = 0; M[q, b, :, i] = 0
                if v == 1:
                    for w, e, m in ((0, 3, 1), (2, 3, 1), (4, 3, 1), (6, 5, 1), (7, 7, 1), (8, 7, 0), (9, 7, 1), (10, 7, 0), (11, 7, 1), (12, 7, 0), (13, 7, 0), (14, 7, 0)):
                        E[q, b, w, i] = e; M[q, b, w, i] = m
                elif v == 2:
                    E[q, b, k, i] = W - 3; M[q, b, k, i] = 1
                elif v == 3:
                    E[q, b, k, i] = 11; M[q, b, k, i] = 1; E[q, b, k + 1, i] = 7
                else:
                    E[q, b, k, i] = (1001, 13, 17)[v - 4]; M[q, b, k, i] = 1
    return pack(X, E, M)
def check_inputs(d):
    bad = []
    for k, lo, hi in (("xt", 0, 255), ("led", 0, W - 1), ("mk", 0, 1)):
        v = np.asarray(d[k]).astype(np.float64)
        if np.min(v) < lo or np.max(v) > hi or np.any(v != np.floor(v)): bad.append("range of " + k)
    return bad
def look(X, ix):
    return np.take_along_axis(X, ix.reshape(N, 8, 1, 16 * P), 3).reshape(N, 8, 16, 16, P)
def reference(xt, led, mk):
    X = xt.astype(np.float32).astype(np.int64).reshape(N, 8, 16, W)
    E = led.astype(np.int64).reshape(N, 8, 16, A); M = mk.astype(np.float32).astype(np.int64).reshape(N, 8, 16, A)
    kappa = np.zeros((N, 1, 1, 1), np.int64); ks = np.arange(16).reshape(1, 1, 16, 1)
    for t in range(RO):
        c = t % S; e = E[:, :, :, c::S].copy(); m = M[:, :, :, c::S].copy()
        x = look(X, e); q = x.copy(); b = np.zeros((N, 8, 16, P), np.int64)
        for k in range(16):
            mm = m[:, :, k][:, :, None, :]
            if k % 2 == 0: b = b + mm * x[:, :, :, k]
            else:
                q[:, :, :, k] = np.minimum(b, x[:, :, :, k]); b = b - mm * q[:, :, :, k]
        u = np.add.reduce(WT.reshape(1, 1, 16, 1, 1) * q, axis=2) & (W - 1)
        h = (((e * u) >> 5) + e + kappa) & (W - 1)
        g = np.add.reduce(np.sign(look(X, h) - q), axis=2); over = np.add.reduce((q > 0).astype(np.int64), axis=2)
        con = (over >= 9) & (((m == 1) & (g < 0)) | ((m == 0) & (g > 0)))
        best = np.argmax(np.where(con, np.abs(g), 0), axis=2)
        flip = np.any(con, axis=2)
        win = flip[:, :, None, :] & (ks == best[:, :, None, :])
        E[:, :, :, c::S] = np.where(win, h, e); M[:, :, :, c::S] = np.where(win, 1 - m, m)
        f = flip.astype(np.int64); kappa = (np.add.reduce(f.reshape(N, 8 * P), axis=1) & 31).reshape(N, 1, 1, 1)
        place = np.add.accumulate(f, axis=2) - 1; go = flip & (place < CAP)
        qb = np.take_along_axis(q, best[:, :, None, None, :], 3)[:, :, :, 0]; ub = np.take_along_axis(u, best[:, :, None, :], 2)[:, :, 0]
        new = X.copy()
        for r in range(N):
            d = (r + 1 + t % (N - 1)) % N
            for v in range(8):
                i = np.flatnonzero(go[r, v]); col = BL * place[r, v, i] + (ub[r, v, i] & (BL - 1))
                new[d, v][:, col] = (X[d, v][:, col] + qb[r, v][:, i]) >> 1
        X = new
    return {"yx": X.reshape(N, 128, W).astype(np.float32).astype(BF), "yl": E.reshape(N, 128, A).astype(np.float32), "ym": M.reshape(N, 128, A).astype(np.float32).astype(BF)}

@@ -1,0 +1,535 @@
+from concourse.bass import DstId, RemoteDMATransfer
+from concourse.mybir import dt, AluOpType, AxisListType, ActivationFunctionType
+
+OP = AluOpType
+AF = ActivationFunctionType
+RO = 5
+XC = 16
+XW = XC + 512 * 32
+
+SCRATCH = {
+    "xw": ("sbuf", [128, XW], "bfloat16"),
+    "ei0": ("sbuf", [128, 1024], "int32"),
+    "ef": ("sbuf", [128, 1024], "float32"),
+    "mm": ("sbuf", [128, 1024], "bfloat16"),
+    "sgn": ("sbuf", [128, 1024], "bfloat16"),
+    "ylb": ("sbuf", [128, 1024], "float32"),
+    "d0": ("sbuf", [128, 4096], "bfloat16"),
+    "bb": ("sbuf", [128, 4096], "bfloat16"),
+    "qq": ("sbuf", [128, 4096], "bfloat16"),
+    "dq": ("sbuf", [128, 4096], "bfloat16"),
+    "sg": ("sbuf", [128, 4096], "bfloat16"),
+    "ov": ("sbuf", [128, 4096], "bfloat16"),
+    "yb": ("sbuf", [128, 1024], "bfloat16"),
+    "alt": ("sbuf", [128, 2048], "bfloat16"),
+    "dl16": ("sbuf", [128, 256], "uint16"),
+    "el16": ("sbuf", [128, 256], "uint16"),
+    "h16": ("sbuf", [128, 256], "uint16"),
+    "ei": ("sbuf", [128, 256], "int32"),
+    "ek": ("sbuf", [128, 256], "int32"),
+    "ui": ("sbuf", [128, 256], "int32"),
+    "ua": ("sbuf", [128, 256], "int32"),
+    "ta": ("sbuf", [128, 256], "int32"),
+    "tb": ("sbuf", [128, 256], "int32"),
+    "tc": ("sbuf", [128, 256], "int32"),
+    "hh": ("sbuf", [128, 256], "int32"),
+    "hf": ("sbuf", [128, 256], "float32"),
+    "de": ("sbuf", [128, 256], "float32"),
+    "td": ("sbuf", [128, 256], "float32"),
+    "tm": ("sbuf", [128, 256], "bfloat16"),
+    "av": ("sbuf", [128, 256], "float32"),
+    "ai": ("sbuf", [128, 256], "int32"),
+    "pi": ("sbuf", [128, 1], "int32"),
+    "ci": ("sbuf", [128, 8], "int32"),
+    "cf": ("sbuf", [128, 32], "float32"),
+    "m1": ("sbuf", [128, 160], "float32"),
+    "si": ("sbuf", [128, 128], "float32"),
+    "clf": ("sbuf", [128, 8], "float32"),
+    "cl": ("sbuf", [128, 8], "uint16"),
+    "icf": ("sbuf", [128, 16], "float32"),
+    "icn": ("sbuf", [128, 16], "bfloat16"),
+    "icr": ("sbuf", [128, 16], "bfloat16"),
+    "i16": ("sbuf", [128, 16], "int32"),
+    "mg": ("sbuf", [128, 128], "float32"),
+    "idn": ("sbuf", [128, 128], "bfloat16"),
+    "nid": ("sbuf", [128, 128], "bfloat16"),
+    "nk": ("sbuf", [128, 128], "bfloat16"),
+    "g8": ("sbuf", [128, 8], "bfloat16"),
+    "rcp": ("sbuf", [128, 8], "bfloat16"),
+    "wu": ("sbuf", [128, 144], "bfloat16"),
+    "pm": ("sbuf", [128, 512], "float32"),
+    "iv": ("sbuf", [128, 512], "float32"),
+    "nbl": ("sbuf", [128, 128], "bfloat16"),
+    "lt": ("sbuf", [128, 128], "bfloat16"),
+    "t1": ("sbuf", [128, 128], "bfloat16"),
+    "am": ("sbuf", [128, 128], "bfloat16"),
+    "one": ("sbuf", [128, 128], "bfloat16"),
+    "mr": ("sbuf", [128, 128], "bfloat16"),
+    "ke": ("sbuf", [128, 128], "bfloat16"),
+    "z16": ("sbuf", [128, 16], "bfloat16"),
+    "ge": ("sbuf", [128, 256], "bfloat16"),
+    "gsg": ("sbuf", [128, 256], "bfloat16"),
+    "sgt": ("sbuf", [128, 256], "bfloat16"),
+    "kt0": ("sbuf", [128, 128], "bfloat16"),
+    "kt1": ("sbuf", [128, 128], "bfloat16"),
+    "sc0": ("sbuf", [128, 128], "bfloat16"),
+    "sc1": ("sbuf", [128, 128], "bfloat16"),
+    "lm0": ("sbuf", [128, 128], "bfloat16"),
+    "lm1": ("sbuf", [128, 128], "bfloat16"),
+    "wn0": ("sbuf", [128, 128], "bfloat16"),
+    "wn1": ("sbuf", [128, 128], "bfloat16"),
+    "nf": ("sbuf", [128, 16], "bfloat16"),
+    "nfs": ("sbuf", [128, 32], "bfloat16"),
+    "nfi": ("sbuf", [128, 16], "bfloat16"),
+    "kn": ("sbuf", [128, 16], "int32"),
+    "li": ("sbuf", [128, 16], "int32"),
+    "lj": ("sbuf", [128, 16], "int32"),
+    "l16": ("sbuf", [128, 16], "uint16"),
+    "ofi": ("sbuf", [128, 16], "int32"),
+    "uwi": ("sbuf", [128, 16], "int32"),
+    "uwa": ("sbuf", [128, 16], "int32"),
+    "tgi": ("sbuf", [128, 16], "int32"),
+    "kc": ("sbuf", [128, 1], "float32"),
+    "kci": ("sbuf", [128, 1], "int32"),
+    "kcj": ("sbuf", [128, 1], "int32"),
+    "kap": ("sbuf", [128, 1], "float32"),
+    "p0": ("psum", [128, 512], "float32"),
+    "p1": ("psum", [128, 512], "float32"),
+    "p2": ("psum", [128, 512], "float32"),
+    "p3": ("psum", [128, 512], "float32"),
+    "p4": ("psum", [128, 512], "float32"),
+    "p5": ("psum", [128, 512], "float32"),
+    "p6": ("psum", [128, 512], "float32"),
+    "p7": ("psum", [128, 512], "float32"),
+}
+for _t in range(RO):
+    SCRATCH["qw%d" % _t] = ("sbuf", [128, 256], "bfloat16")
+    SCRATCH["lq%d" % _t] = ("sbuf", [128, 256], "bfloat16")
+    SCRATCH["tg%d" % _t] = ("sbuf", [128, 16], "uint16")
+    SCRATCH["lt%d" % _t] = ("sbuf", [128, 16], "uint16")
+SEMAPHORES = ["cv", "cs", "cp", "cg", "ls"] + ["aq%d" % _t for _t in range(RO)] + ["at%d" % _t for _t in range(RO)] \
+    + ["dm%d" % _t for _t in range(24)]
+
+
+def rank_program(g, core, T, topo):
+    rank = T.rank_of(core)
+    if rank is None:
+        return
+    n_ranks = len(T.cores)
+    eng = {"v": g.vector, "s": g.scalar, "p": g.tensor, "g": g, "y": g.sync}
+    semname = {"v": "cv", "s": "cs", "p": "cp", "g": "cg"}
+    cnt = {"v": 0, "s": 0, "p": 0, "g": 0}
+    value = {}
+    known = {q: {} for q in eng}
+    snap = {}
+    wr, rd, bank = {}, {}, {}
+    ndma = [0]
+
+    def need(q, deps):
+        best = {}
+        for (s, n) in deps:
+            if n > best.get(s, 0):
+                best[s] = n
+        for s in sorted(best, key=lambda s: s not in ("v", "s", "p")):
+            n = best[s]
+            if known[q].get(s, 0) >= n:
+                continue
+            eng[q].wait_ge(T.sem[semname.get(s, s)], value.get((s, n), n))
+            kq = known[q]
+            kq[s] = n
+            for s2, n2 in snap.get((s, n), {}).items():
+                if n2 > kq.get(s2, 0):
+                    kq[s2] = n2
+
+    def deps_of(q, R, W, B):
+        d = []
+        for (b, lo, hi) in R:
+            for (l, h, s, n) in wr.get(b, ()):
+                if l < hi and lo < h:
+                    d.append((s, n))
+        for (b, lo, hi) in W:
+            for (l, h, s, n) in wr.get(b, ()):
+                if l < hi and lo < h:
+                    d.append((s, n))
+            for (l, h, s, n) in rd.get(b, ()):
+                if l < hi and lo < h:
+                    d.append((s, n))
+        for b in B:
+            for s, n in bank.get(b, {}).items():
+                if s != q:
+                    d.append((s, n))
+        return d
+
+    def note(key, R, W, B):
+        s, n = key
+        for (b, lo, hi) in W:
+            wr[b] = [e for e in wr.get(b, ()) if not (lo <= e[0] and e[1] <= hi)] + [(lo, hi, s, n)]
+            rd[b] = [e for e in rd.get(b, ()) if not (lo <= e[0] and e[1] <= hi)]
+        for (b, lo, hi) in R:
+            rd[b] = [e for e in rd.get(b, ()) if not (e[2] == s and lo <= e[0] and e[1] <= hi)] + [(lo, hi, s, n)]
+        for b in B:
+            bank.setdefault(b, {})[s] = n
+
+    def op(q, fn, R, W, B=()):
+        need(q, deps_of(q, R, W, B))
+        cnt[q] += 1
+        key = (q, cnt[q])
+        snap[key] = dict(known[q])
+        fn(eng[q]).then_inc(T.sem[semname[q]], 1)
+        note(key, R, W, B)
+
+    def dma(q, out, in_, R, W):
+        need(q, deps_of(q, R, W, ()))
+        name = "dm%d" % ndma[0]
+        ndma[0] += 1
+        snap[(name, 1)] = dict(known[q])
+        value[(name, 1)] = 16
+        eng[q].dma_start(out, in_).then_inc(T.sem[name], 16)
+        note((name, 1), R, W, ())
+
+    def A(b, lo=0, hi=1 << 20):
+        return (b, lo, hi)
+
+    def mm(out, l, r, st, sp, R, B):
+        op("p", lambda e: e.matmul(out, l, r, st, sp), R, [], B)
+
+    def ts(out, in0, s1, o1, R, W, B=(), s2=None, o2=None):
+        if o2 is None:
+            op("v", lambda e: e.tensor_scalar(out, in0, s1, None, o1), R, W, B)
+        else:
+            op("v", lambda e: e.tensor_scalar(out, in0, s1, s2, o1, o2), R, W, B)
+
+    def tt(out, a, b, o, R, W, B=()):
+        op("v", lambda e: e.tensor_tensor(out, a, b, o), R, W, B)
+
+    def cp(out, in_, R, W, B=()):
+        op("v", lambda e: e.tensor_copy(out, in_), R, W, B)
+
+    def act(out, in_, f, R, W, B=()):
+        op("s", lambda e: e.activation(out, in_, f), R, W, B)
+
+    def fill(ap, c, W):
+        op("v", lambda e: e.memset(ap, c), [], W)
+
+    def iota(ap, pat, base, cm, W, fl=True):
+        if fl:
+            op("g", lambda e: e.iota(ap, pat, base, cm, allow_small_or_imprecise_dtypes=True), [], W)
+        else:
+            op("g", lambda e: e.iota(ap, pat, base, cm), [], W)
+
+    dma("y", T.ei0[:], T.led[:], [], [A("ei0")])
+    dma("s", T.mm[:], T.mk[:], [], [A("mm")])
+    dma("y", T.xw[:, XC:XC + 2048], T.xt[:, 0:2048], [], [A("xw", XC, XC + 2048)])
+    dma("s", T.xw[:, XC + 2048:XC + 4096], T.xt[:, 2048:4096], [], [A("xw", XC + 2048, XC + 4096)])
+    dma("y", T.xw[:, XC + 4096:XC + 8192], T.xt[:], [], [A("xw", XC + 4096, XC + 8192)])
+    dma("s", T.xw[:, XC + 8192:XC + 12288], T.xt[:], [], [A("xw", XC + 8192, XC + 12288)])
+
+    iota(T.pi[:], [[0, 1]], 0, 1, [A("pi")], False)
+    iota(T.m1[:], [[1, 160]], 1, 0, [A("m1")])
+    iota(T.clf[:], [[16, 8]], 15, 0, [A("clf")])
+    iota(T.mg[:], [[16, 8], [0, 16]], 0, 0, [A("mg")])
+    iota(T.si[:], [[0, 8], [1, 16]], 0, 0, [A("si")])
+    iota(T.icf[:], [[16, 16]], 0, 1, [A("icf")])
+    fill(T.xw[:, 0:16], 0.0, [A("xw", 0, 16)])
+    fill(T.xw[:, 1:2], 4096.0, [A("xw", 0, 16)])
+    fill(T.alt[:, 0::2], 4096.0, [A("alt")])
+    fill(T.alt[:, 1::2], 0.0, [A("alt")])
+
+    def ci(j):
+        return T.ci[:, j:j + 1]
+
+    def cf(j):
+        return T.cf[:, j:j + 1]
+
+    def rc(j):
+        return ("cf", j, j + 1)
+    ts(ci(0), T.pi[:], 15, OP.bitwise_and, [A("pi")], [("ci", 0, 1)])
+    ts(ci(1), T.pi[:], 3, OP.logical_shift_right, [A("pi")], [("ci", 1, 2)], (), 1, OP.bitwise_and)
+    ts(ci(2), T.pi[:], 1, OP.bitwise_and, [A("pi")], [("ci", 2, 3)])
+    ts(ci(3), T.pi[:], 1, OP.logical_shift_right, [A("pi")], [("ci", 3, 4)], (), 7, OP.bitwise_and)
+    ts(ci(4), T.pi[:], 7, OP.bitwise_and, [A("pi")], [("ci", 4, 5)])
+    cp(T.cf[:, 0:5], T.ci[:, 0:5], [("ci", 0, 5)], [("cf", 0, 5)])
+    cp(cf(5), T.pi[:], [A("pi")], [rc(5)])
+    tt(cf(6), cf(5), cf(0), OP.subtract, [rc(5), rc(0)], [rc(6)])
+    ts(cf(7), cf(2), -1.0, OP.mult, [rc(2)], [rc(7)], (), 1.0, OP.add)
+    ts(cf(8), cf(1), -1.0, OP.mult, [rc(1)], [rc(8)], (), 1.0, OP.add)
+    tt(cf(9), cf(6), cf(3), OP.add, [rc(6), rc(3)], [rc(9)])
+    ts(cf(10), cf(4), 2.0, OP.mult, [rc(4), rc(6)], [rc(10)], (), cf(6), OP.add)
+    for par in range(2):
+        for b in range(2):
+            j = 11 + 2 * par + b
+            ts(cf(j), cf(9), float(8 * b + 1), OP.add, [rc(9), rc(7), rc(2)], [rc(j)], (), cf(2 if par else 7), OP.mult)
+            j = 15 + 2 * par + b
+            ts(cf(j), cf(10), float(par + 1), OP.add, [rc(10), rc(1), rc(8)], [rc(j)], (), cf(1 if b else 8), OP.mult)
+    for j in range(4):
+        ts(T.pm[:, 128 * j:128 * j + 128], T.m1[:, 0:128], cf(11 + j), OP.is_equal, [A("m1"), rc(11 + j)], [("pm", 128 * j, 128 * j + 128)])
+    ts(cf(19), cf(0), 14.5, OP.is_lt, [rc(0)], [rc(19)])
+    ts(cf(20), cf(0), 14.5, OP.is_gt, [rc(0)], [rc(20)])
+
+    def early_lists(c):
+        ts(T.ef[:, c::4], T.ei0[:, c::4], 16.0, OP.add, [A("ei0")], [("ef%d" % c, 0, 1)])
+
+    def prep_x(c):
+        for par in range(2):
+            for b in range(2):
+                j = 2 * par + b
+                mm(T.p0[:, 128 * par:128 * par + 128], T.pm[:, 128 * j:128 * j + 128], T.ef[:, c + 4 * b::8], b == 0, b == 1,
+                   [("pm", 128 * j, 128 * j + 128), A("ef%d" % c)], [0])
+        tt(T.td[:], T.ef[:, c::4], T.mm[:, c::4], OP.mult, [A("ef%d" % c), A("mm")], [A("td")])
+        ts(T.dl16[:], T.td[:], cf(19), OP.mult, [A("td"), rc(19), rc(20)], [A("dl16")], (), cf(20), OP.add)
+        cp(T.el16[:], T.p0[:, 0:256], [], [A("el16")], [0])
+        ts(T.ei[:], T.p0[:, 0:256], -16.0, OP.add, [], [A("ei")], [0])
+
+    def prep_s(c):
+        ts(T.sgn[:, c::4], T.mm[:, c::4], -2.0, OP.mult, [A("mm")], [A("sgn")], (), 1.0, OP.add)
+        for H in range(2):
+            mm(T.p3[:, 256 + 128 * H:384 + 128 * H], T.sgn[:, 512 * H + c:512 * H + 512:4], T.idn[:], True, True, [A("sgn"), A("idn")], [3])
+        cp(T.sgt[:], T.p3[:, 256:512], [], [A("sgt")], [3])
+
+    early_lists(0)
+    prep_x(0)
+    ts(cf(21), cf(0), 2.0, OP.mult, [rc(0)], [rc(21)], (), 1.0, OP.add)
+    ts(cf(22), cf(6), 16.0, OP.add, [rc(6)], [rc(22)])
+    ts(cf(23), cf(0), -1.0, OP.mult, [rc(0)], [rc(23)])
+    ts(cf(25), cf(6), 0.0625, OP.mult, [rc(6)], [rc(25)], (), 1.0, OP.add)
+    ts(cf(26), cf(5), 1.0, OP.add, [rc(5)], [rc(26)])
+    ts(T.wu[:], T.m1[:, 0:144], cf(22), OP.is_equal, [A("m1"), rc(22), rc(21)], [A("wu")], (), cf(21), OP.mult)
+    ts(T.idn[:], T.m1[:, 0:128], cf(26), OP.is_equal, [A("m1"), rc(26)], [A("idn")])
+    ts(T.nid[:], T.m1[:, 0:128], cf(26), OP.is_equal, [A("m1"), rc(26)], [A("nid")], (), -1.0, OP.mult)
+    ts(T.nk[:], T.m1[:, 0:128], cf(26), OP.is_equal, [A("m1"), rc(26), rc(23)], [A("nk")], (), cf(23), OP.mult)
+    ts(T.g8[:], T.m1[:, 0:8], cf(25), OP.is_equal, [A("m1"), rc(25)], [A("g8")], (), 16.0, OP.mult)
+
+    def late_constants():
+        ts(T.rcp[:], T.m1[:, 0:8], cf(25), OP.is_equal, [A("m1"), rc(25)], [A("rcp")])
+        ts(T.nbl[:], T.mg[:], cf(6), OP.is_equal, [A("mg"), rc(6)], [A("nbl")], (), -1.0, OP.mult)
+        ts(T.lt[:], T.m1[:, 0:128], cf(26), OP.is_gt, [A("m1"), rc(26)], [A("lt")])
+        tt(T.t1[:], T.nbl[:], T.lt[:], OP.mult, [A("nbl"), A("lt")], [A("t1")])
+        ts(T.lt[:], T.idn[:], 256.0, OP.mult, [A("idn")], [A("lt")])
+        tt(T.am[:], T.lt[:], T.t1[:], OP.add, [A("lt"), A("t1")], [A("am")])
+        ts(T.icf[:], T.icf[:], cf(6), OP.subtract, [A("icf"), rc(6)], [A("icf")])
+        cp(T.icn[:], T.icf[:], [A("icf")], [A("icn")])
+        ts(T.icr[:], T.icf[:], -1.0, OP.mult, [A("icf")], [A("icr")], (), 255.0, OP.add)
+        ts(T.i16[:], T.icf[:], 16.0, OP.mult, [A("icf")], [A("i16")])
+        ts(T.mr[:], T.si[:], cf(0), OP.is_equal, [A("si"), rc(0)], [A("mr")])
+        cp(T.cl[:], T.clf[:], [A("clf")], [A("cl")])
+        fill(T.ke[:], 512.0, [A("ke")])
+        fill(T.ke[:, 0::16], 0.5, [A("ke")])
+        fill(T.z16[:], 0.0, [A("z16")])
+        fill(T.nfs[:], 0.0, [A("nfs")])
+        fill(T.one[:], 1.0, [A("one")])
+        for j in range(4):
+            ts(T.iv[:, 128 * j:128 * j + 128], T.m1[:, 0:128], cf(15 + j), OP.is_equal, [A("m1"), rc(15 + j)], [A("iv")])
+        fill(T.xw[:, XC + 12288:XC + 16384], 0.0, [A("xw", XC + 12288, XC + 16384)])
+
+    items = T.xw[:, XC:XC + 4096]
+    all_x = T.xw[:, 0:XC + 4096]
+    RX = ("xw", 0, XC + 4096)
+
+    def gather_even(q, H):
+        out = T.qq[:, 2048 * H:2048 * H + 2048:2]
+        src = all_x.indirect(T.el16[:, 64 * H:64 * H + 64])
+        if q == "v":
+            cp(out, src, [RX, A("el16")], [("qe", H, H + 1)])
+        else:
+            act(out, src, AF.Copy, [RX, A("el16")], [("qe", H, H + 1)])
+
+    def gather_d(H):
+        act(T.d0[:, 2048 * H:2048 * H + 2048], all_x.indirect(T.dl16[:, 128 * H:128 * H + 128]), AF.Copy,
+            [RX, A("dl16")], [("d0", H, H + 1)])
+
+    def hashes(H, par, ps, col, B):
+        for r in range(16):
+            mm(ps[:, col:col + 64], T.wu[:, 15 - r:143 - r], T.qq[:, 2048 * H + 2 * r + par:2048 * H + 2048:32], r == 0, r == 15,
+               [A("wu"), ("qo" if par else "qe", H, H + 1)], [B])
+
+    def hop(lo, hi, src, B, first):
+        s = slice(lo, hi)
+        def rg(b):
+            return (b, lo, hi)
+        cp(T.ui[:, s], src, [], [rg("ui")], [B])
+        ts(T.ua[:, s], T.ui[:, s], 4095, OP.bitwise_and, [rg("ui")], [rg("ua")])
+        tt(T.ta[:, s], T.ei[:, s], T.ua[:, s], OP.mult, [A("ei"), rg("ua")], [rg("ta")])
+        ts(T.tb[:, s], T.ta[:, s], 5, OP.logical_shift_right, [rg("ta")], [rg("tb")])
+        e, en = (T.ei, "ei") if first else (T.ek, "ek")
+        tt(T.tc[:, s], T.tb[:, s], e[:, s], OP.add, [rg("tb"), A(en)], [rg("tc")])
+        ts(T.hh[:, s], T.tc[:, s], 4095, OP.bitwise_and, [rg("tc")], [rg("hh")])
+        cp(T.h16[:, s], T.hh[:, s], [rg("hh")], [rg("h16")])
+
+    def scan(H):
+        s = slice(2048 * H, 2048 * H + 2048)
+        op("v", lambda e: e.tensor_tensor_scan(T.bb[:, s], T.d0[:, s], T.alt[:], 0.0, OP.subtract, OP.min),
+           [("d0", H, H + 1), A("alt")], [("bb", H, H + 1)])
+
+    def odd_min(H):
+        tt(T.qq[:, 2048 * H + 1:2048 * H + 2048:2], all_x.indirect(T.el16[:, 128 + 64 * H:192 + 64 * H]),
+           T.bb[:, 2048 * H:2048 * H + 2048:2], OP.min, [RX, A("el16"), ("bb", H, H + 1)], [("qo", H, H + 1)])
+
+    def look(H, par):
+        s = slice(2048 * H + par, 2048 * H + 2048, 2)
+        lo = 128 * par + 64 * H
+        tt(T.dq[:, s], items.indirect(T.h16[:, lo:lo + 64]), T.qq[:, s], OP.subtract,
+           [RX, ("h16", lo, lo + 64), ("qo" if par else "qe", H, H + 1)], [("dq", 2 * H + par, 2 * H + par + 1)])
+        ts(T.sg[:, s], T.dq[:, s], 1.0, OP.min, [("dq", 2 * H + par, 2 * H + par + 1)], [("sg", 2 * H + par, 2 * H + par + 1)], (), -1.0, OP.max)
+
+    def score(H, par, c):
+        ps, B = (T.p7, 7) if H else (T.p6, 6)
+        if par == 0:
+            mm(ps[:, 0:128], T.sgn[:, 512 * H + c:512 * H + 512:4], T.nk[:], True, False, [A("sgn"), A("nk")], [B])
+        for k in range(par, 16, 2):
+            mm(ps[:, k:128:16], T.sg[:, 2048 * H + k:2048 * H + 2048:16], T.g8[:], False, k == 15,
+               [("sg", 2 * H + par, 2 * H + par + 1), A("g8")], [B])
+
+    def over(H):
+        act(T.ov[:, 2048 * H:2048 * H + 2048], T.qq[:, 2048 * H:2048 * H + 2048], AF.Sign,
+            [("qe", H, H + 1), ("qo", H, H + 1)], [("ov", H, H + 1)])
+        for k in range(16):
+            mm(T.p3[:, 128 * H + k:128 * H + 128:16], T.ov[:, 2048 * H + k:2048 * H + 2048:16], T.g8[:], True, True, [("ov", H, H + 1), A("g8")], [3])
+
+    def gate(H):
+        s = slice(128 * H, 128 * H + 128)
+        ts(T.ge[:, s], T.p3[:, s], 136.0, OP.is_gt, [], [("ge", H, H + 1)], [3])
+        tt(T.gsg[:, s], T.ge[:, s], T.sgt[:, s], OP.mult, [("ge", H, H + 1), A("sgt")], [("gsg", H, H + 1)])
+
+    def keys(H):
+        ps, B = (T.p7, 7) if H else (T.p6, 6)
+        kt, sc = T["kt%d" % H], T["sc%d" % H]
+        tt(kt[:], ps[:, 0:128], T.gsg[:, 128 * H:128 * H + 128], OP.mult, [("gsg", H, H + 1)], [A("kt%d" % H)], [B])
+        op("v", lambda e: e.tensor_tensor_scan(sc[:], T.ke[:], kt[:], 0.5, OP.min, OP.max), [A("ke"), A("kt%d" % H)], [A("sc%d" % H)])
+        lm = T["lm%d" % H]
+        tt(lm[:], sc[:].indirect(T.cl[:]), T.mr[:], OP.mult, [A("sc%d" % H), A("cl"), A("mr")], [A("lm%d" % H)])
+        mm(T.p4[:, 8 * H:8 * H + 8], lm[:], T.rcp[:], True, True, [A("lm%d" % H), A("rcp")], [4])
+
+    nloc = [0]
+    for t in range(RO):
+        c = t % 4
+        first = t == 0
+        gather_even("s", 0)
+        gather_even("v", 1)
+        gather_d(0)
+        gather_d(1)
+        hashes(0, 0, T.p0, 0, 0)
+        hashes(1, 0, T.p0, 64, 0)
+        if first:
+            prep_s(0)
+            late_constants()
+        hop(0, 128, T.p0[:, 0:128], 0, first)
+        act(T.yb[:], items.indirect(T.h16[:, 64:128]), AF.Copy, [RX, ("h16", 64, 128)], [A("yb")])
+        for z in range(2):
+            ps, B = (T.p5, 5) if z else (T.p4, 4)
+            mm(ps[:], T.idn[:], T.yb[:, 512 * z:512 * z + 512], True, False, [A("idn"), A("yb")], [B])
+            mm(ps[:], T.nid[:], T.qq[:, 2048 + 1024 * z:3072 + 1024 * z:2], False, True, [A("nid"), ("qe", 1, 2)], [B])
+        look(0, 0)
+        scan(0)
+        odd_min(0)
+        hashes(0, 1, T.p1, 0, 1)
+        scan(1)
+        odd_min(1)
+        hashes(1, 1, T.p2, 0, 2)
+        hop(128, 192, T.p1[:, 0:64], 1, first)
+        over(0)
+        for z in range(2):
+            ps, B = (T.p5, 5) if z else (T.p4, 4)
+            act(T.sg[:, 2048 + 1024 * z:3072 + 1024 * z:2], ps[:], AF.Sign, [], [("sg", 2, 3)], [B])
+        over(1)
+        score(0, 0, c)
+        look(0, 1)
+        score(0, 1, c)
+        hop(192, 256, T.p2[:, 0:64], 2, first)
+        gate(0)
+        look(1, 1)
+        gate(1)
+        keys(0)
+        score(1, 0, c)
+        score(1, 1, c)
+        keys(1)
+        kl = T.p4[:, 0:16]
+        mm(T.p5[:, 0:16], T.idn[:], T.icn[:], True, False, [A("idn"), A("icn")], [5])
+        ts(T.kn[:], kl, -1.0, OP.mult, [], [A("kn")], [4])
+        ts(T.nf[:], kl, 0.75, OP.is_lt, [], [A("nf")], [4])
+        ts(T.li[:], T.kn[:], 15, OP.bitwise_and, [A("kn")], [A("li")])
+        op("v", lambda e: e.tensor_tensor_scan(T.nfs[:, 1:17], T.nf[:], T.z16[:], 0.0, OP.add, OP.max), [A("nf"), A("z16")], [A("nfs")])
+        tt(T.lj[:], T.li[:], T.i16[:], OP.add, [A("li"), A("i16")], [A("lj")])
+        tt(T.nfi[:], T.nf[:], T.icr[:], OP.mult, [A("nf"), A("icr")], [A("nfi")])
+        cp(T.l16[:], T.lj[:], [A("lj")], [A("l16")])
+        mm(T.p5[:, 0:16], T.am[:], T.nf[:], False, False, [A("am"), A("nf")], [5])
+        mm(T.p5[:, 0:16], T.nbl[:], T.nfs[:, 0:16], False, False, [A("nbl"), A("nfs")], [5])
+        mm(T.p5[:, 0:16], T.idn[:], T.nfi[:], False, True, [A("idn"), A("nfi")], [5])
+        qw, qn = T["qw%d" % t], "qw%d" % t
+        cp(qw[:], T.qq[:].indirect(T.l16[:]), [A("qe"), A("qo"), A("l16")], [A(qn)])
+        for r in range(16):
+            mm(T.p1[:, 0:16], T.wu[:, 15 - r:143 - r], qw[:, r::16], r == 0, r == 15, [A("wu"), A(qn)], [1])
+        ts(T.ofi[:], T.p5[:, 0:16], 32.0, OP.mult, [], [A("ofi")], [5])
+        cp(T.uwi[:], T.p1[:, 0:16], [], [A("uwi")], [1])
+        ts(T.uwa[:], T.uwi[:], 31, OP.bitwise_and, [A("uwi")], [A("uwa")])
+        tt(T.tgi[:], T.uwa[:], T.ofi[:], OP.add, [A("uwa"), A("ofi")], [A("tgi")])
+        cp(T["tg%d" % t][:], T.tgi[:], [A("tgi")], [A("tg%d" % t)])
+        dst = T.cores[(rank + 1 + t % (n_ranks - 1)) % n_ranks]
+        es = topo.engines(core, dst)[:8]
+        mask = sum(1 << e for e in es)
+        rid, pid, _ = topo.addr(dst)
+        src = T.cores[(rank - 1 - t % (n_ranks - 1)) % n_ranks]
+        n_in = len(topo.engines(src, core)[:8])
+        for a, b, sm in (("qw", "lq", "aq"), ("tg", "lt", "at")):
+            need("g", deps_of("g", [A("%s%d" % (a, t))], [], ()))
+            g.remote_dma(T["%s%d" % (b, t)][:], T["%s%d" % (a, t)][:], T.sem["%s%d" % (sm, t)], T.sem.ls, pid, rid, mask)
+            nloc[0] += len(es)
+            value[("%s%d" % (sm, t), 1)] = n_in
+            note(("%s%d" % (sm, t), 1), [], [A("%s%d" % (b, t))], ())
+        if t < RO - 1:
+            mm(T.p5[:, 32:48], T.one[:], T.nf[:], True, True, [A("one"), A("nf")], [5])
+            op("v", lambda e: e.tensor_reduce(T.kc[:], T.p5[:, 32:48], AxisListType.X, OP.add), [], [A("kc")], [5])
+            ts(T.kci[:], T.kc[:], -1.0, OP.mult, [A("kc")], [A("kci")])
+            ts(T.kcj[:], T.kci[:], 31, OP.bitwise_and, [A("kci")], [A("kcj")])
+            cp(T.kap[:], T.kcj[:], [A("kcj")], [A("kap")])
+            if t < 3:
+                early_lists(t + 1)
+                prep_x((t + 1) % 4)
+                prep_s((t + 1) % 4)
+                ts(T.ek[:], T.ei[:], T.kap[:], OP.add, [A("ei"), A("kap")], [A("ek")])
+
+        def update():
+            ts(T.hf[:], T.hh[:], 16.0, OP.add, [A("hh")], [A("hf")])
+            for b in range(2):
+                for par in range(2):
+                    j = 2 * par + b
+                    mm(T.p2[:, 128 * b:128 * b + 128], T.iv[:, 128 * j:128 * j + 128], T.hf[:, 128 * par:128 * par + 128], par == 0, par == 1,
+                       [A("iv"), A("hf")], [2])
+            for H in range(2):
+                kt, sc, wn = T["kt%d" % H], T["sc%d" % H], T["wn%d" % H]
+                tt(wn[:], sc[:].indirect(T.cl[:]), kt[:], OP.is_equal, [A("kt%d" % H), A("cl"), A("sc%d" % H)], [A("wn%d" % H)])
+                mm(T.p5[:, 128 + 128 * H:256 + 128 * H], wn[:], T.idn[:], True, True, [A("wn%d" % H), A("idn")], [5])
+            R = A("ef%d" % c)
+            for b in range(2):
+                d = T.de[:, 128 * b:128 * b + 128]
+                e = T.ef[:, c + 4 * b::8]
+                rg = ("de", b, b + 1)
+                tt(d, T.p2[:, 128 * b:128 * b + 128], e, OP.subtract, [R], [rg], [2])
+                tt(d, T.p5[:, 128 + b:384:2], d, OP.mult, [rg], [rg], [5])
+                tt(e, e, d, OP.add, [R, rg], [("ef%d" % c, b, b + 1)])
+            tt(T.tm[:], T.p5[:, 128:384], T.sgn[:, c::4], OP.mult, [A("sgn")], [A("tm")], [5])
+            tt(T.mm[:, c::4], T.mm[:, c::4], T.tm[:], OP.add, [A("mm"), A("tm")], [A("mm")])
+        if t < 3:
+            update()
+        elif t == 3:
+            prep_x(0)
+            prep_s(0)
+            ts(T.ek[:], T.ei[:], T.kap[:], OP.add, [A("ei"), A("kap")], [A("ek")])
+            update()
+        else:
+            update()
+            dma("y", T.ym[:], T.mm[:], [A("mm")], [])
+            ts(T.ylb[:], T.ef[:], -16.0, OP.add, [A("ef0"), A("ef1"), A("ef2"), A("ef3")], [A("ylb")])
+            dma("s", T.yl[:], T.ylb[:], [A("ylb")], [])
+        win = T.xw[:, XC:XW]
+        WX = ("xw", XC, XW)
+        lt = T["lt%d" % t]
+        tt(T.av[:], win.indirect(lt[:]), T["lq%d" % t][:], OP.add, [WX, A("lt%d" % t), A("lq%d" % t)], [A("av")])
+        ts(T.ai[:], T.av[:], 0.5, OP.mult, [A("av")], [A("ai")], (), -0.25, OP.add)
+        cp(win.indirect(lt[:]), T.ai[:], [A("ai"), A("lt%d" % t)], [WX])
+    dma("y", T.yx[:, 0:2048], T.xw[:, XC:XC + 2048], [WX], [])
+    dma("s", T.yx[:, 2048:4096], T.xw[:, XC + 2048:XC + 4096], [WX], [])
+    for q in ("v", "s", "p", "g"):
+        g.wait_ge(T.sem[semname[q]], cnt[q])
+    for j in range(ndma[0]):
+        g.wait_ge(T.sem["dm%d" % j], 16)
+    g.wait_ge(T.sem.ls, nloc[0])

@@ -6,102 +6,31 @@ AF = ActivationFunctionType
 RO = 5
 XC = 16
 XW = XC + 512 * 32
+LOOK_S = ((0, 0), (0, 1))
+EVEN_V = (0, 1)
 
-SCRATCH = {
-    "xw": ("sbuf", [128, XW], "bfloat16"),
-    "ei0": ("sbuf", [128, 1024], "int32"),
-    "ef": ("sbuf", [128, 1024], "float32"),
-    "mm": ("sbuf", [128, 1024], "bfloat16"),
-    "sgn": ("sbuf", [128, 1024], "bfloat16"),
-    "ylb": ("sbuf", [128, 1024], "float32"),
-    "d0": ("sbuf", [128, 4096], "bfloat16"),
-    "bb": ("sbuf", [128, 4096], "bfloat16"),
-    "qq": ("sbuf", [128, 4096], "bfloat16"),
-    "dq": ("sbuf", [128, 4096], "bfloat16"),
-    "sg": ("sbuf", [128, 4096], "bfloat16"),
-    "ov": ("sbuf", [128, 4096], "bfloat16"),
-    "yb": ("sbuf", [128, 1024], "bfloat16"),
-    "alt": ("sbuf", [128, 2048], "bfloat16"),
-    "dl16": ("sbuf", [128, 256], "uint16"),
-    "el16": ("sbuf", [128, 256], "uint16"),
-    "h16": ("sbuf", [128, 256], "uint16"),
-    "ei": ("sbuf", [128, 256], "int32"),
-    "ek": ("sbuf", [128, 256], "int32"),
-    "ui": ("sbuf", [128, 256], "int32"),
-    "ua": ("sbuf", [128, 256], "int32"),
-    "ta": ("sbuf", [128, 256], "int32"),
-    "tb": ("sbuf", [128, 256], "int32"),
-    "tc": ("sbuf", [128, 256], "int32"),
-    "hh": ("sbuf", [128, 256], "int32"),
-    "hf": ("sbuf", [128, 256], "float32"),
-    "de": ("sbuf", [128, 256], "float32"),
-    "td": ("sbuf", [128, 256], "float32"),
-    "tm": ("sbuf", [128, 256], "bfloat16"),
-    "av": ("sbuf", [128, 256], "float32"),
-    "ai": ("sbuf", [128, 256], "int32"),
-    "pi": ("sbuf", [128, 1], "int32"),
-    "ci": ("sbuf", [128, 8], "int32"),
-    "cf": ("sbuf", [128, 32], "float32"),
-    "m1": ("sbuf", [128, 160], "float32"),
-    "si": ("sbuf", [128, 128], "float32"),
-    "clf": ("sbuf", [128, 8], "float32"),
-    "cl": ("sbuf", [128, 8], "uint16"),
-    "icf": ("sbuf", [128, 16], "float32"),
-    "icn": ("sbuf", [128, 16], "bfloat16"),
-    "icr": ("sbuf", [128, 16], "bfloat16"),
-    "i16": ("sbuf", [128, 16], "int32"),
-    "mg": ("sbuf", [128, 128], "float32"),
-    "idn": ("sbuf", [128, 128], "bfloat16"),
-    "nid": ("sbuf", [128, 128], "bfloat16"),
-    "nk": ("sbuf", [128, 128], "bfloat16"),
-    "g8": ("sbuf", [128, 8], "bfloat16"),
-    "rcp": ("sbuf", [128, 8], "bfloat16"),
-    "wu": ("sbuf", [128, 144], "bfloat16"),
-    "pm": ("sbuf", [128, 512], "float32"),
-    "iv": ("sbuf", [128, 512], "float32"),
-    "nbl": ("sbuf", [128, 128], "bfloat16"),
-    "lt": ("sbuf", [128, 128], "bfloat16"),
-    "t1": ("sbuf", [128, 128], "bfloat16"),
-    "am": ("sbuf", [128, 128], "bfloat16"),
-    "one": ("sbuf", [128, 128], "bfloat16"),
-    "mr": ("sbuf", [128, 128], "bfloat16"),
-    "ke": ("sbuf", [128, 128], "bfloat16"),
-    "z16": ("sbuf", [128, 16], "bfloat16"),
-    "ge": ("sbuf", [128, 256], "bfloat16"),
-    "gsg": ("sbuf", [128, 256], "bfloat16"),
-    "sgt": ("sbuf", [128, 256], "bfloat16"),
-    "kt0": ("sbuf", [128, 128], "bfloat16"),
-    "kt1": ("sbuf", [128, 128], "bfloat16"),
-    "sc0": ("sbuf", [128, 128], "bfloat16"),
-    "sc1": ("sbuf", [128, 128], "bfloat16"),
-    "lm0": ("sbuf", [128, 128], "bfloat16"),
-    "lm1": ("sbuf", [128, 128], "bfloat16"),
-    "wn0": ("sbuf", [128, 128], "bfloat16"),
-    "wn1": ("sbuf", [128, 128], "bfloat16"),
-    "nf": ("sbuf", [128, 16], "bfloat16"),
-    "nfs": ("sbuf", [128, 32], "bfloat16"),
-    "nfi": ("sbuf", [128, 16], "bfloat16"),
-    "kn": ("sbuf", [128, 16], "int32"),
-    "li": ("sbuf", [128, 16], "int32"),
-    "lj": ("sbuf", [128, 16], "int32"),
-    "l16": ("sbuf", [128, 16], "uint16"),
-    "ofi": ("sbuf", [128, 16], "int32"),
-    "uwi": ("sbuf", [128, 16], "int32"),
-    "uwa": ("sbuf", [128, 16], "int32"),
-    "tgi": ("sbuf", [128, 16], "int32"),
-    "kc": ("sbuf", [128, 1], "float32"),
-    "kci": ("sbuf", [128, 1], "int32"),
-    "kcj": ("sbuf", [128, 1], "int32"),
-    "kap": ("sbuf", [128, 1], "float32"),
-    "p0": ("psum", [128, 512], "float32"),
-    "p1": ("psum", [128, 512], "float32"),
-    "p2": ("psum", [128, 512], "float32"),
-    "p3": ("psum", [128, 512], "float32"),
-    "p4": ("psum", [128, 512], "float32"),
-    "p5": ("psum", [128, 512], "float32"),
-    "p6": ("psum", [128, 512], "float32"),
-    "p7": ("psum", [128, 512], "float32"),
-}
+SCRATCH = {"xw": ("sbuf", [128, XW], "bfloat16"), "alt": ("sbuf", [128, 2048], "bfloat16")}
+for _n, _w, _d in (
+        ("ei0", 1024, "int32"), ("ef", 1024, "float32"), ("mm", 1024, "bfloat16"), ("sgn", 1024, "bfloat16"), ("ylb", 1024, "float32"),
+        ("d0", 4096, "bfloat16"), ("bb", 4096, "bfloat16"), ("qq", 4096, "bfloat16"), ("dq", 4096, "bfloat16"), ("sg", 4096, "bfloat16"),
+        ("ov", 4096, "bfloat16"), ("yb", 4096, "bfloat16"),
+        ("dl16", 256, "uint16"), ("el16", 256, "uint16"), ("h16", 256, "uint16"), ("ei", 256, "int32"), ("ek", 256, "int32"),
+        ("ui", 256, "int32"), ("ua", 256, "int32"), ("ta", 256, "int32"), ("tb", 256, "int32"), ("tc", 256, "int32"), ("hh", 256, "int32"),
+        ("hf", 256, "float32"), ("de", 256, "float32"), ("td", 256, "float32"), ("tm", 256, "bfloat16"), ("av", 256, "float32"), ("ai", 256, "int32"),
+        ("pi", 1, "int32"), ("ci", 8, "int32"), ("cf", 32, "float32"), ("m1", 160, "float32"), ("si", 128, "float32"), ("clf", 8, "float32"),
+        ("cl", 8, "uint16"), ("icf", 16, "float32"), ("icn", 16, "bfloat16"), ("icr", 16, "bfloat16"), ("i16", 16, "int32"), ("mg", 128, "float32"),
+        ("idn", 128, "bfloat16"), ("nid", 128, "bfloat16"), ("nk", 128, "bfloat16"), ("g8", 8, "bfloat16"), ("rcp", 8, "bfloat16"),
+        ("wu", 144, "bfloat16"), ("pm", 512, "float32"), ("iv", 512, "float32"), ("nbl", 128, "bfloat16"), ("lt", 128, "bfloat16"),
+        ("idx", 128, "bfloat16"), ("t1", 128, "bfloat16"), ("am", 128, "bfloat16"), ("one", 128, "bfloat16"), ("mr", 128, "bfloat16"),
+        ("ke", 128, "bfloat16"), ("z16", 16, "bfloat16"),
+        ("ge", 256, "bfloat16"), ("gsg", 256, "bfloat16"), ("sgt", 256, "bfloat16"), ("kt0", 128, "bfloat16"), ("kt1", 128, "bfloat16"),
+        ("sc0", 128, "bfloat16"), ("sc1", 128, "bfloat16"), ("lm0", 128, "bfloat16"), ("lm1", 128, "bfloat16"), ("wn0", 128, "bfloat16"),
+        ("wn1", 128, "bfloat16"), ("nf", 16, "bfloat16"), ("nfs", 32, "bfloat16"), ("nfi", 16, "bfloat16"), ("kn", 16, "int32"), ("li", 16, "int32"),
+        ("lj", 16, "int32"), ("l16", 16, "uint16"), ("ofi", 16, "int32"), ("uwi", 16, "int32"), ("uwa", 16, "int32"), ("tgi", 16, "int32"),
+        ("kc", 1, "float32"), ("kci", 1, "int32"), ("kcj", 1, "int32"), ("kap", 1, "float32")):
+    SCRATCH[_n] = ("sbuf", [128, _w], _d)
+for _t in range(8):
+    SCRATCH["p%d" % _t] = ("psum", [128, 512], "float32")
 for _t in range(RO):
     SCRATCH["qw%d" % _t] = ("sbuf", [128, 256], "bfloat16")
     SCRATCH["lq%d" % _t] = ("sbuf", [128, 256], "bfloat16")
@@ -109,6 +38,11 @@ for _t in range(RO):
     SCRATCH["lt%d" % _t] = ("sbuf", [128, 16], "uint16")
 SEMAPHORES = ["cv", "cs", "cp", "cg", "ls"] + ["aq%d" % _t for _t in range(RO)] + ["at%d" % _t for _t in range(RO)] \
     + ["dm%d" % _t for _t in range(24)]
+
+PASSES = 12
+CYC = 0.001
+GAT = 0.00150
+SCA = 0.0030
 
 
 def rank_program(g, core, T, topo):
@@ -118,122 +52,109 @@ def rank_program(g, core, T, topo):
     n_ranks = len(T.cores)
     eng = {"v": g.vector, "s": g.scalar, "p": g.tensor, "g": g, "y": g.sync}
     semname = {"v": "cv", "s": "cs", "p": "cp", "g": "cg"}
-    cnt = {"v": 0, "s": 0, "p": 0, "g": 0}
-    value = {}
-    known = {q: {} for q in eng}
-    snap = {}
+
+    nodes = []
     wr, rd, bank = {}, {}, {}
     ndma = [0]
 
-    def need(q, deps):
-        best = {}
-        for (s, n) in deps:
-            if n > best.get(s, 0):
-                best[s] = n
-        for s in sorted(best, key=lambda s: s not in ("v", "s", "p")):
-            n = best[s]
-            if known[q].get(s, 0) >= n:
-                continue
-            eng[q].wait_ge(T.sem[semname.get(s, s)], value.get((s, n), n))
-            kq = known[q]
-            kq[s] = n
-            for s2, n2 in snap.get((s, n), {}).items():
-                if n2 > kq.get(s2, 0):
-                    kq[s2] = n2
-
-    def deps_of(q, R, W, B):
-        d = []
+    def node(q, calls, cost, R, W, B=(), kind="c", key=None, late=0.0, extra=()):
+        d = set(extra)
         for (b, lo, hi) in R:
-            for (l, h, s, n) in wr.get(b, ()):
+            for (l, h, i) in wr.get(b, ()):
                 if l < hi and lo < h:
-                    d.append((s, n))
+                    d.add(i)
         for (b, lo, hi) in W:
-            for (l, h, s, n) in wr.get(b, ()):
+            for (l, h, i) in wr.get(b, ()):
                 if l < hi and lo < h:
-                    d.append((s, n))
-            for (l, h, s, n) in rd.get(b, ()):
+                    d.add(i)
+            for (l, h, i) in rd.get(b, ()):
                 if l < hi and lo < h:
-                    d.append((s, n))
+                    d.add(i)
+        me = len(nodes)
+        order = set()
         for b in B:
-            for s, n in bank.get(b, {}).items():
-                if s != q:
-                    d.append((s, n))
-        return d
-
-    def note(key, R, W, B):
-        s, n = key
+            if b in bank:
+                (order if nodes[bank[b]]["q"] == q else d).add(bank[b])
+                for j in nodes[bank[b]]["chain"].get(b, ()):
+                    if nodes[j]["q"] != q:
+                        d.add(j)
+        chain = {}
+        for b in B:
+            last = {}
+            if b in bank:
+                for j in nodes[bank[b]]["chain"].get(b, ()):
+                    last[nodes[j]["q"]] = j
+                last[nodes[bank[b]]["q"]] = bank[b]
+            chain[b] = list(last.values())
+        nodes.append({"q": q, "calls": calls, "cost": cost, "deps": d, "order": order - d, "kind": kind, "key": key, "late": late, "chain": chain})
+        for b in B:
+            bank[b] = me
         for (b, lo, hi) in W:
-            wr[b] = [e for e in wr.get(b, ()) if not (lo <= e[0] and e[1] <= hi)] + [(lo, hi, s, n)]
+            wr[b] = [e for e in wr.get(b, ()) if not (lo <= e[0] and e[1] <= hi)] + [(lo, hi, me)]
             rd[b] = [e for e in rd.get(b, ()) if not (lo <= e[0] and e[1] <= hi)]
         for (b, lo, hi) in R:
-            rd[b] = [e for e in rd.get(b, ()) if not (e[2] == s and lo <= e[0] and e[1] <= hi)] + [(lo, hi, s, n)]
-        for b in B:
-            bank.setdefault(b, {})[s] = n
+            rd.setdefault(b, []).append((lo, hi, me))
+        return me
 
-    def op(q, fn, R, W, B=()):
-        need(q, deps_of(q, R, W, B))
-        cnt[q] += 1
-        key = (q, cnt[q])
-        snap[key] = dict(known[q])
-        fn(eng[q]).then_inc(T.sem[semname[q]], 1)
-        note(key, R, W, B)
-
-    def dma(q, out, in_, R, W):
-        need(q, deps_of(q, R, W, ()))
+    def dma(q, out, in_, R, W, by):
         name = "dm%d" % ndma[0]
         ndma[0] += 1
-        snap[(name, 1)] = dict(known[q])
-        value[(name, 1)] = 16
-        eng[q].dma_start(out, in_).then_inc(T.sem[name], 16)
-        note((name, 1), R, W, ())
+        node(q, [lambda e: e.dma_start(out, in_)], 0.1, R, W, (), "d", name, 2.0 + by * 4e-6)
 
     def A(b, lo=0, hi=1 << 20):
         return (b, lo, hi)
 
-    def mm(out, l, r, st, sp, R, B):
-        op("p", lambda e: e.matmul(out, l, r, st, sp), R, [], B)
+    def cy(n):
+        return max(64, n) * CYC
 
-    def ts(out, in0, s1, o1, R, W, B=(), s2=None, o2=None):
+    def mms(lst, n, R, B):
+        node("p", [lambda e, a=a: e.matmul(*a) for a in lst], len(lst) * n * CYC, R, [], B)
+
+    def ts(out, in0, s1, o1, R, W, B=(), s2=None, o2=None, n=64):
         if o2 is None:
-            op("v", lambda e: e.tensor_scalar(out, in0, s1, None, o1), R, W, B)
+            node("v", [lambda e: e.tensor_scalar(out, in0, s1, None, o1)], cy(n), R, W, B)
         else:
-            op("v", lambda e: e.tensor_scalar(out, in0, s1, s2, o1, o2), R, W, B)
+            node("v", [lambda e: e.tensor_scalar(out, in0, s1, s2, o1, o2)], cy(n), R, W, B)
 
-    def tt(out, a, b, o, R, W, B=()):
-        op("v", lambda e: e.tensor_tensor(out, a, b, o), R, W, B)
+    def tt(out, a, b, o, R, W, B=(), n=64, cost=None):
+        node("v", [lambda e: e.tensor_tensor(out, a, b, o)], cost or cy(n), R, W, B)
 
-    def cp(out, in_, R, W, B=()):
-        op("v", lambda e: e.tensor_copy(out, in_), R, W, B)
+    def cp(out, in_, R, W, B=(), n=64, cost=None):
+        node("v", [lambda e: e.tensor_copy(out, in_)], cost or cy(n), R, W, B)
 
-    def act(out, in_, f, R, W, B=()):
-        op("s", lambda e: e.activation(out, in_, f), R, W, B)
+    def scn(out, a, b, init, o1, o2, R, W, n):
+        node("v", [lambda e: e.tensor_tensor_scan(out, a, b, init, o1, o2)], cy(n), R, W)
 
-    def fill(ap, c, W):
-        op("v", lambda e: e.memset(ap, c), [], W)
+    def act(out, in_, f, R, W, B=(), n=64, cost=None, **kw):
+        node("s", [lambda e: e.activation(out, in_, f, **kw)], cost or cy(n), R, W, B)
 
-    def iota(ap, pat, base, cm, W, fl=True):
+    def fill(ap, c, W, n=64):
+        node("v", [lambda e: e.memset(ap, c)], cy(n), [], W)
+
+    def iota(ap, pat, base, cm, W, n, fl=True):
         if fl:
-            op("g", lambda e: e.iota(ap, pat, base, cm, allow_small_or_imprecise_dtypes=True), [], W)
+            node("g", [lambda e: e.iota(ap, pat, base, cm, allow_small_or_imprecise_dtypes=True)], 0.13 + 2 * n * CYC, [], W)
         else:
-            op("g", lambda e: e.iota(ap, pat, base, cm), [], W)
+            node("g", [lambda e: e.iota(ap, pat, base, cm)], 0.13 + 2 * n * CYC, [], W)
 
-    dma("y", T.ei0[:], T.led[:], [], [A("ei0")])
-    dma("s", T.mm[:], T.mk[:], [], [A("mm")])
-    dma("y", T.xw[:, XC:XC + 2048], T.xt[:, 0:2048], [], [A("xw", XC, XC + 2048)])
-    dma("s", T.xw[:, XC + 2048:XC + 4096], T.xt[:, 2048:4096], [], [A("xw", XC + 2048, XC + 4096)])
-    dma("y", T.xw[:, XC + 4096:XC + 8192], T.xt[:], [], [A("xw", XC + 4096, XC + 8192)])
-    dma("s", T.xw[:, XC + 8192:XC + 12288], T.xt[:], [], [A("xw", XC + 8192, XC + 12288)])
+    MM4 = [A("mm%d" % c) for c in range(4)]
+    dma("y", T.ei0[:], T.led[:], [], [A("ei0")], 524288)
+    dma("s", T.mm[:], T.mk[:], [], MM4, 262144)
+    dma("y", T.xw[:, XC:XC + 2048], T.xt[:, 0:2048], [], [A("xw", XC, XC + 2048)], 1048576)
+    dma("s", T.xw[:, XC + 2048:XC + 4096], T.xt[:, 2048:4096], [], [A("xw", XC + 2048, XC + 4096)], 1048576)
+    dma("y", T.xw[:, XC + 4096:XC + 8192], T.xt[:], [], [A("xw", XC + 4096, XC + 8192)], 2500000)
+    dma("s", T.xw[:, XC + 8192:XC + 12288], T.xt[:], [], [A("xw", XC + 8192, XC + 12288)], 2500000)
 
-    iota(T.pi[:], [[0, 1]], 0, 1, [A("pi")], False)
-    iota(T.m1[:], [[1, 160]], 1, 0, [A("m1")])
-    iota(T.clf[:], [[16, 8]], 15, 0, [A("clf")])
-    iota(T.mg[:], [[16, 8], [0, 16]], 0, 0, [A("mg")])
-    iota(T.si[:], [[0, 8], [1, 16]], 0, 0, [A("si")])
-    iota(T.icf[:], [[16, 16]], 0, 1, [A("icf")])
+    iota(T.pi[:], [[0, 1]], 0, 1, [A("pi")], 1, False)
+    iota(T.m1[:], [[1, 160]], 1, 0, [A("m1")], 160)
+    iota(T.clf[:], [[16, 8]], 15, 0, [A("clf")], 8)
+    iota(T.mg[:], [[16, 8], [0, 16]], 0, 0, [A("mg")], 128)
+    iota(T.si[:], [[0, 8], [1, 16]], 0, 0, [A("si")], 128)
+    iota(T.icf[:], [[16, 16]], 0, 1, [A("icf")], 16)
     fill(T.xw[:, 0:16], 0.0, [A("xw", 0, 16)])
     fill(T.xw[:, 1:2], 4096.0, [A("xw", 0, 16)])
-    fill(T.alt[:, 0::2], 4096.0, [A("alt")])
-    fill(T.alt[:, 1::2], 0.0, [A("alt")])
+    fill(T.alt[:, 0::2], 4096.0, [A("alt", 0, 1)], 512)
+    fill(T.alt[:, 1::2], 0.0, [A("alt", 1, 2)], 512)
 
     def ci(j):
         return T.ci[:, j:j + 1]
@@ -262,207 +183,148 @@ def rank_program(g, core, T, topo):
             j = 15 + 2 * par + b
             ts(cf(j), cf(10), float(par + 1), OP.add, [rc(10), rc(1), rc(8)], [rc(j)], (), cf(1 if b else 8), OP.mult)
     for j in range(4):
-        ts(T.pm[:, 128 * j:128 * j + 128], T.m1[:, 0:128], cf(11 + j), OP.is_equal, [A("m1"), rc(11 + j)], [("pm", 128 * j, 128 * j + 128)])
+        ts(T.pm[:, 128 * j:128 * j + 128], T.m1[:, 0:128], cf(11 + j), OP.is_equal, [A("m1"), rc(11 + j)], [("pm", j, j + 1)], n=128)
+        ts(T.iv[:, 128 * j:128 * j + 128], T.m1[:, 0:128], cf(15 + j), OP.is_equal, [A("m1"), rc(15 + j)], [("iv", j, j + 1)], n=128)
     ts(cf(19), cf(0), 14.5, OP.is_lt, [rc(0)], [rc(19)])
     ts(cf(20), cf(0), 14.5, OP.is_gt, [rc(0)], [rc(20)])
-
-    def early_lists(c):
-        ts(T.ef[:, c::4], T.ei0[:, c::4], 16.0, OP.add, [A("ei0")], [("ef%d" % c, 0, 1)])
-
-    def prep_x(c):
-        for par in range(2):
-            for b in range(2):
-                j = 2 * par + b
-                mm(T.p0[:, 128 * par:128 * par + 128], T.pm[:, 128 * j:128 * j + 128], T.ef[:, c + 4 * b::8], b == 0, b == 1,
-                   [("pm", 128 * j, 128 * j + 128), A("ef%d" % c)], [0])
-        tt(T.td[:], T.ef[:, c::4], T.mm[:, c::4], OP.mult, [A("ef%d" % c), A("mm")], [A("td")])
-        ts(T.dl16[:], T.td[:], cf(19), OP.mult, [A("td"), rc(19), rc(20)], [A("dl16")], (), cf(20), OP.add)
-        cp(T.el16[:], T.p0[:, 0:256], [], [A("el16")], [0])
-        ts(T.ei[:], T.p0[:, 0:256], -16.0, OP.add, [], [A("ei")], [0])
-
-    def prep_s(c):
-        ts(T.sgn[:, c::4], T.mm[:, c::4], -2.0, OP.mult, [A("mm")], [A("sgn")], (), 1.0, OP.add)
-        for H in range(2):
-            mm(T.p3[:, 256 + 128 * H:384 + 128 * H], T.sgn[:, 512 * H + c:512 * H + 512:4], T.idn[:], True, True, [A("sgn"), A("idn")], [3])
-        cp(T.sgt[:], T.p3[:, 256:512], [], [A("sgt")], [3])
-
-    early_lists(0)
-    prep_x(0)
     ts(cf(21), cf(0), 2.0, OP.mult, [rc(0)], [rc(21)], (), 1.0, OP.add)
     ts(cf(22), cf(6), 16.0, OP.add, [rc(6)], [rc(22)])
     ts(cf(23), cf(0), -1.0, OP.mult, [rc(0)], [rc(23)])
     ts(cf(25), cf(6), 0.0625, OP.mult, [rc(6)], [rc(25)], (), 1.0, OP.add)
     ts(cf(26), cf(5), 1.0, OP.add, [rc(5)], [rc(26)])
-    ts(T.wu[:], T.m1[:, 0:144], cf(22), OP.is_equal, [A("m1"), rc(22), rc(21)], [A("wu")], (), cf(21), OP.mult)
-    ts(T.idn[:], T.m1[:, 0:128], cf(26), OP.is_equal, [A("m1"), rc(26)], [A("idn")])
-    ts(T.nid[:], T.m1[:, 0:128], cf(26), OP.is_equal, [A("m1"), rc(26)], [A("nid")], (), -1.0, OP.mult)
-    ts(T.nk[:], T.m1[:, 0:128], cf(26), OP.is_equal, [A("m1"), rc(26), rc(23)], [A("nk")], (), cf(23), OP.mult)
+    ts(T.wu[:], T.m1[:, 0:144], cf(22), OP.is_equal, [A("m1"), rc(22), rc(21)], [A("wu")], (), cf(21), OP.mult, n=144)
+    ts(T.idn[:], T.m1[:, 0:128], cf(26), OP.is_equal, [A("m1"), rc(26)], [A("idn")], n=128)
+    ts(T.nid[:], T.m1[:, 0:128], cf(26), OP.is_equal, [A("m1"), rc(26)], [A("nid")], (), -1.0, OP.mult, n=128)
+    ts(T.idx[:], T.m1[:, 0:128], cf(26), OP.is_equal, [A("m1"), rc(26)], [A("idx")], (), 256.0, OP.mult, n=128)
+    ts(T.nk[:], T.m1[:, 0:128], cf(26), OP.is_equal, [A("m1"), rc(26), rc(23)], [A("nk")], (), cf(23), OP.mult, n=128)
     ts(T.g8[:], T.m1[:, 0:8], cf(25), OP.is_equal, [A("m1"), rc(25)], [A("g8")], (), 16.0, OP.mult)
+    ts(T.rcp[:], T.m1[:, 0:8], cf(25), OP.is_equal, [A("m1"), rc(25)], [A("rcp")])
+    ts(T.nbl[:], T.mg[:], cf(6), OP.is_equal, [A("mg"), rc(6)], [A("nbl")], (), -1.0, OP.mult, n=128)
+    ts(T.lt[:], T.m1[:, 0:128], cf(26), OP.is_gt, [A("m1"), rc(26)], [A("lt")], n=128)
+    tt(T.t1[:], T.nbl[:], T.lt[:], OP.mult, [A("nbl"), A("lt")], [A("t1")], n=256)
+    tt(T.am[:], T.idx[:], T.t1[:], OP.add, [A("idx"), A("t1")], [A("am")], n=256)
+    ts(T.icf[:], T.icf[:], cf(6), OP.subtract, [A("icf"), rc(6)], [A("icf")])
+    cp(T.icn[:], T.icf[:], [A("icf")], [A("icn")])
+    ts(T.icr[:], T.icf[:], -1.0, OP.mult, [A("icf")], [A("icr")], (), 255.0, OP.add)
+    ts(T.i16[:], T.icf[:], 16.0, OP.mult, [A("icf")], [A("i16")])
+    ts(T.mr[:], T.si[:], cf(0), OP.is_equal, [A("si"), rc(0)], [A("mr")], n=128)
+    cp(T.cl[:], T.clf[:], [A("clf")], [A("cl")])
+    fill(T.ke[:], 512.0, [A("ke")])
+    fill(T.ke[:, 0::16], 0.5, [A("ke")])
+    fill(T.z16[:], 0.0, [A("z16")])
+    fill(T.nfs[:], 0.0, [A("nfs")])
+    fill(T.one[:], 1.0, [A("one")])
+    for z in range(4):
+        lo = XC + 12288 + 1024 * z
+        fill(T.xw[:, lo:lo + 1024], 0.0, [A("xw", lo, lo + 1024)], 512)
 
-    def late_constants():
-        ts(T.rcp[:], T.m1[:, 0:8], cf(25), OP.is_equal, [A("m1"), rc(25)], [A("rcp")])
-        ts(T.nbl[:], T.mg[:], cf(6), OP.is_equal, [A("mg"), rc(6)], [A("nbl")], (), -1.0, OP.mult)
-        ts(T.lt[:], T.m1[:, 0:128], cf(26), OP.is_gt, [A("m1"), rc(26)], [A("lt")])
-        tt(T.t1[:], T.nbl[:], T.lt[:], OP.mult, [A("nbl"), A("lt")], [A("t1")])
-        ts(T.lt[:], T.idn[:], 256.0, OP.mult, [A("idn")], [A("lt")])
-        tt(T.am[:], T.lt[:], T.t1[:], OP.add, [A("lt"), A("t1")], [A("am")])
-        ts(T.icf[:], T.icf[:], cf(6), OP.subtract, [A("icf"), rc(6)], [A("icf")])
-        cp(T.icn[:], T.icf[:], [A("icf")], [A("icn")])
-        ts(T.icr[:], T.icf[:], -1.0, OP.mult, [A("icf")], [A("icr")], (), 255.0, OP.add)
-        ts(T.i16[:], T.icf[:], 16.0, OP.mult, [A("icf")], [A("i16")])
-        ts(T.mr[:], T.si[:], cf(0), OP.is_equal, [A("si"), rc(0)], [A("mr")])
-        cp(T.cl[:], T.clf[:], [A("clf")], [A("cl")])
-        fill(T.ke[:], 512.0, [A("ke")])
-        fill(T.ke[:, 0::16], 0.5, [A("ke")])
-        fill(T.z16[:], 0.0, [A("z16")])
-        fill(T.nfs[:], 0.0, [A("nfs")])
-        fill(T.one[:], 1.0, [A("one")])
-        for j in range(4):
-            ts(T.iv[:, 128 * j:128 * j + 128], T.m1[:, 0:128], cf(15 + j), OP.is_equal, [A("m1"), rc(15 + j)], [A("iv")])
-        fill(T.xw[:, XC + 12288:XC + 16384], 0.0, [A("xw", XC + 12288, XC + 16384)])
+    def early_lists(c):
+        ts(T.ef[:, c::4], T.ei0[:, c::4], 16.0, OP.add, [A("ei0")], [A("ef%d" % c)], n=256)
+
+    def prep_x(c):
+        E, M = A("ef%d" % c), A("mm%d" % c)
+        tt(T.td[:], T.ef[:, c::4], T.mm[:, c::4], OP.mult, [E, M], [A("td")], n=512)
+        ts(T.dl16[:], T.td[:], cf(19), OP.mult, [A("td"), rc(19), rc(20)], [A("dl16")], (), cf(20), OP.add, n=256)
+        for par in range(2):
+            mms([(T.p0[:, 128 * par:128 * par + 128], T.pm[:, 256 * par + 128 * b:256 * par + 128 * b + 128], T.ef[:, c + 4 * b::8], b == 0, b == 1)
+                 for b in range(2)], 512, [A("pm"), E], [0])
+        cp(T.el16[:], T.p0[:, 0:256], [], [A("el16")], [0], n=256)
+        ts(T.ei[:], T.p0[:, 0:256], -16.0, OP.add, [], [A("ei")], [0], n=256)
+
+    def prep_s(c):
+        act(T.sgn[:, c::4], T.mm[:, c::4], AF.Copy, [A("mm%d" % c)], [A("sgn%d" % c)], n=256, scale=-2.0, bias=1.0)
+        mms([(T.p3[:, 256 + 128 * H:384 + 128 * H], T.sgn[:, 512 * H + c:512 * H + 512:4], T.idn[:], True, True) for H in range(2)],
+            128, [A("sgn%d" % c), A("idn")], [3])
+        act(T.sgt[:], T.p3[:, 256:512], AF.Copy, [], [A("sgt")], [3], n=256)
 
     items = T.xw[:, XC:XC + 4096]
     all_x = T.xw[:, 0:XC + 4096]
     RX = ("xw", 0, XC + 4096)
 
-    def gather_even(q, H):
+    def gather_even(H):
         out = T.qq[:, 2048 * H:2048 * H + 2048:2]
         src = all_x.indirect(T.el16[:, 64 * H:64 * H + 64])
-        if q == "v":
-            cp(out, src, [RX, A("el16")], [("qe", H, H + 1)])
-        else:
-            act(out, src, AF.Copy, [RX, A("el16")], [("qe", H, H + 1)])
+        f = cp if H in EVEN_V else (lambda o, i, R, W, cost: act(o, i, AF.Copy, R, W, cost=cost))
+        f(out, src, [RX, A("el16")], [("qe", H, H + 1)], cost=0.06 + 1024 * GAT)
 
     def gather_d(H):
         act(T.d0[:, 2048 * H:2048 * H + 2048], all_x.indirect(T.dl16[:, 128 * H:128 * H + 128]), AF.Copy,
-            [RX, A("dl16")], [("d0", H, H + 1)])
+            [RX, A("dl16")], [("d0", H, H + 1)], cost=0.06 + 2048 * GAT)
 
     def hashes(H, par, ps, col, B):
-        for r in range(16):
-            mm(ps[:, col:col + 64], T.wu[:, 15 - r:143 - r], T.qq[:, 2048 * H + 2 * r + par:2048 * H + 2048:32], r == 0, r == 15,
-               [A("wu"), ("qo" if par else "qe", H, H + 1)], [B])
+        mms([(ps[:, col:col + 64], T.wu[:, 15 - r:143 - r], T.qq[:, 2048 * H + 2 * r + par:2048 * H + 2048:32], r == 0, r == 15) for r in range(16)],
+            64, [A("wu"), ("qo" if par else "qe", H, H + 1)], [B])
 
     def hop(lo, hi, src, B, first):
         s = slice(lo, hi)
+        n = hi - lo
+
         def rg(b):
             return (b, lo, hi)
-        cp(T.ui[:, s], src, [], [rg("ui")], [B])
-        ts(T.ua[:, s], T.ui[:, s], 4095, OP.bitwise_and, [rg("ui")], [rg("ua")])
-        tt(T.ta[:, s], T.ei[:, s], T.ua[:, s], OP.mult, [A("ei"), rg("ua")], [rg("ta")])
-        ts(T.tb[:, s], T.ta[:, s], 5, OP.logical_shift_right, [rg("ta")], [rg("tb")])
+        cp(T.ui[:, s], src, [], [rg("ui")], [B], n=n)
+        ts(T.ua[:, s], T.ui[:, s], 4095, OP.bitwise_and, [rg("ui")], [rg("ua")], n=n)
+        tt(T.ta[:, s], T.ei[:, s], T.ua[:, s], OP.mult, [A("ei"), rg("ua")], [rg("ta")], n=2 * n)
+        ts(T.tb[:, s], T.ta[:, s], 5, OP.logical_shift_right, [rg("ta")], [rg("tb")], n=n)
         e, en = (T.ei, "ei") if first else (T.ek, "ek")
-        tt(T.tc[:, s], T.tb[:, s], e[:, s], OP.add, [rg("tb"), A(en)], [rg("tc")])
-        ts(T.hh[:, s], T.tc[:, s], 4095, OP.bitwise_and, [rg("tc")], [rg("hh")])
-        cp(T.h16[:, s], T.hh[:, s], [rg("hh")], [rg("h16")])
+        tt(T.tc[:, s], T.tb[:, s], e[:, s], OP.add, [rg("tb"), A(en)], [rg("tc")], n=2 * n)
+        ts(T.hh[:, s], T.tc[:, s], 4095, OP.bitwise_and, [rg("tc")], [rg("hh")], n=n)
+        cp(T.h16[:, s], T.hh[:, s], [rg("hh")], [rg("h16")], n=n)
 
     def scan(H):
         s = slice(2048 * H, 2048 * H + 2048)
-        op("v", lambda e: e.tensor_tensor_scan(T.bb[:, s], T.d0[:, s], T.alt[:], 0.0, OP.subtract, OP.min),
-           [("d0", H, H + 1), A("alt")], [("bb", H, H + 1)])
+        scn(T.bb[:, s], T.d0[:, s], T.alt[:], 0.0, OP.subtract, OP.min, [("d0", H, H + 1), A("alt")], [("bb", H, H + 1)], 1024)
 
     def odd_min(H):
         tt(T.qq[:, 2048 * H + 1:2048 * H + 2048:2], all_x.indirect(T.el16[:, 128 + 64 * H:192 + 64 * H]),
-           T.bb[:, 2048 * H:2048 * H + 2048:2], OP.min, [RX, A("el16"), ("bb", H, H + 1)], [("qo", H, H + 1)])
+           T.bb[:, 2048 * H:2048 * H + 2048:2], OP.min, [RX, A("el16"), ("bb", H, H + 1)], [("qo", H, H + 1)], cost=0.06 + 1024 * GAT)
 
     def look(H, par):
         s = slice(2048 * H + par, 2048 * H + 2048, 2)
         lo = 128 * par + 64 * H
+        z = 2 * H + par
+        Q = ("qo" if par else "qe", H, H + 1)
+        if (H, par) in LOOK_S:
+            act(T.yb[:, 1024 * z:1024 * z + 1024], items.indirect(T.h16[:, lo:lo + 64]), AF.Copy, [RX, ("h16", lo, lo + 64)], [("yb", z, z + 1)],
+                cost=0.07 + 1024 * GAT)
+            for x in range(2):
+                ps, B = (T.p5, 5) if x else (T.p4, 4)
+                qs = slice(2048 * H + par + 1024 * x, 2048 * H + 1024 * x + 1024, 2)
+                mms([(ps[:], T.idn[:], T.yb[:, 1024 * z + 512 * x:1024 * z + 512 * x + 512], True, False),
+                     (ps[:], T.nid[:], T.qq[:, qs], False, True)], 512, [A("idn"), A("nid"), ("yb", z, z + 1), Q], [B])
+                act(T.sg[:, qs], ps[:], AF.Sign, [], [("sg", 4 * H + 2 * par + x, 4 * H + 2 * par + x + 1)], [B], n=512)
+            return
         tt(T.dq[:, s], items.indirect(T.h16[:, lo:lo + 64]), T.qq[:, s], OP.subtract,
-           [RX, ("h16", lo, lo + 64), ("qo" if par else "qe", H, H + 1)], [("dq", 2 * H + par, 2 * H + par + 1)])
-        ts(T.sg[:, s], T.dq[:, s], 1.0, OP.min, [("dq", 2 * H + par, 2 * H + par + 1)], [("sg", 2 * H + par, 2 * H + par + 1)], (), -1.0, OP.max)
+           [RX, ("h16", lo, lo + 64), Q], [("dq", z, z + 1)], cost=0.06 + 1024 * GAT)
+        ts(T.sg[:, s], T.dq[:, s], 1.0, OP.min, [("dq", z, z + 1)], [("sg", 2 * z, 2 * z + 2)], (), -1.0, OP.max, n=512)
 
     def score(H, par, c):
         ps, B = (T.p7, 7) if H else (T.p6, 6)
         if par == 0:
-            mm(ps[:, 0:128], T.sgn[:, 512 * H + c:512 * H + 512:4], T.nk[:], True, False, [A("sgn"), A("nk")], [B])
-        for k in range(par, 16, 2):
-            mm(ps[:, k:128:16], T.sg[:, 2048 * H + k:2048 * H + 2048:16], T.g8[:], False, k == 15,
-               [("sg", 2 * H + par, 2 * H + par + 1), A("g8")], [B])
+            mms([(ps[:, 0:128], T.sgn[:, 512 * H + c:512 * H + 512:4], T.nk[:], True, False)], 128, [A("sgn%d" % c), A("nk")], [B])
+        z = 2 * H + par
+        mms([(ps[:, k:128:16], T.sg[:, 2048 * H + k:2048 * H + 2048:16], T.g8[:], False, k == 15) for k in range(par, 16, 2)],
+            64, [("sg", 2 * z, 2 * z + 2), A("g8")], [B])
 
     def over(H):
         act(T.ov[:, 2048 * H:2048 * H + 2048], T.qq[:, 2048 * H:2048 * H + 2048], AF.Sign,
-            [("qe", H, H + 1), ("qo", H, H + 1)], [("ov", H, H + 1)])
-        for k in range(16):
-            mm(T.p3[:, 128 * H + k:128 * H + 128:16], T.ov[:, 2048 * H + k:2048 * H + 2048:16], T.g8[:], True, True, [("ov", H, H + 1), A("g8")], [3])
+            [("qe", H, H + 1), ("qo", H, H + 1)], [("ov", H, H + 1)], n=2048)
+        mms([(T.p3[:, 128 * H + k:128 * H + 128:16], T.ov[:, 2048 * H + k:2048 * H + 2048:16], T.g8[:], True, True) for k in range(16)],
+            64, [("ov", H, H + 1), A("g8")], [3])
 
     def gate(H):
         s = slice(128 * H, 128 * H + 128)
-        ts(T.ge[:, s], T.p3[:, s], 136.0, OP.is_gt, [], [("ge", H, H + 1)], [3])
-        tt(T.gsg[:, s], T.ge[:, s], T.sgt[:, s], OP.mult, [("ge", H, H + 1), A("sgt")], [("gsg", H, H + 1)])
+        ts(T.ge[:, s], T.p3[:, s], 136.0, OP.is_gt, [], [("ge", H, H + 1)], [3], n=128)
+        tt(T.gsg[:, s], T.ge[:, s], T.sgt[:, s], OP.mult, [("ge", H, H + 1), A("sgt")], [("gsg", H, H + 1)], n=256)
 
     def keys(H):
         ps, B = (T.p7, 7) if H else (T.p6, 6)
-        kt, sc = T["kt%d" % H], T["sc%d" % H]
-        tt(kt[:], ps[:, 0:128], T.gsg[:, 128 * H:128 * H + 128], OP.mult, [("gsg", H, H + 1)], [A("kt%d" % H)], [B])
-        op("v", lambda e: e.tensor_tensor_scan(sc[:], T.ke[:], kt[:], 0.5, OP.min, OP.max), [A("ke"), A("kt%d" % H)], [A("sc%d" % H)])
-        lm = T["lm%d" % H]
-        tt(lm[:], sc[:].indirect(T.cl[:]), T.mr[:], OP.mult, [A("sc%d" % H), A("cl"), A("mr")], [A("lm%d" % H)])
-        mm(T.p4[:, 8 * H:8 * H + 8], lm[:], T.rcp[:], True, True, [A("lm%d" % H), A("rcp")], [4])
+        kt, sc, lm = T["kt%d" % H], T["sc%d" % H], T["lm%d" % H]
+        tt(kt[:], ps[:, 0:128], T.gsg[:, 128 * H:128 * H + 128], OP.mult, [("gsg", H, H + 1)], [A("kt%d" % H)], [B], n=128)
+        scn(sc[:], T.ke[:], kt[:], 0.5, OP.min, OP.max, [A("ke"), A("kt%d" % H)], [A("sc%d" % H)], 64)
+        tt(lm[:], sc[:].indirect(T.cl[:]), T.mr[:], OP.mult, [A("sc%d" % H), A("cl"), A("mr")], [A("lm%d" % H)], cost=0.25)
+        mms([(T.p4[:, 8 * H:8 * H + 8], lm[:], T.rcp[:], True, True)], 64, [A("lm%d" % H), A("rcp")], [4])
 
-    nloc = [0]
-    for t in range(RO):
-        c = t % 4
-        first = t == 0
-        gather_even("s", 0)
-        gather_even("v", 1)
-        gather_d(0)
-        gather_d(1)
-        hashes(0, 0, T.p0, 0, 0)
-        hashes(1, 0, T.p0, 64, 0)
-        if first:
-            prep_s(0)
-            late_constants()
-        hop(0, 128, T.p0[:, 0:128], 0, first)
-        act(T.yb[:], items.indirect(T.h16[:, 64:128]), AF.Copy, [RX, ("h16", 64, 128)], [A("yb")])
-        for z in range(2):
-            ps, B = (T.p5, 5) if z else (T.p4, 4)
-            mm(ps[:], T.idn[:], T.yb[:, 512 * z:512 * z + 512], True, False, [A("idn"), A("yb")], [B])
-            mm(ps[:], T.nid[:], T.qq[:, 2048 + 1024 * z:3072 + 1024 * z:2], False, True, [A("nid"), ("qe", 1, 2)], [B])
-        look(0, 0)
-        scan(0)
-        odd_min(0)
-        hashes(0, 1, T.p1, 0, 1)
-        scan(1)
-        odd_min(1)
-        hashes(1, 1, T.p2, 0, 2)
-        hop(128, 192, T.p1[:, 0:64], 1, first)
-        over(0)
-        for z in range(2):
-            ps, B = (T.p5, 5) if z else (T.p4, 4)
-            act(T.sg[:, 2048 + 1024 * z:3072 + 1024 * z:2], ps[:], AF.Sign, [], [("sg", 2, 3)], [B])
-        over(1)
-        score(0, 0, c)
-        look(0, 1)
-        score(0, 1, c)
-        hop(192, 256, T.p2[:, 0:64], 2, first)
-        gate(0)
-        look(1, 1)
-        gate(1)
-        keys(0)
-        score(1, 0, c)
-        score(1, 1, c)
-        keys(1)
-        kl = T.p4[:, 0:16]
-        mm(T.p5[:, 0:16], T.idn[:], T.icn[:], True, False, [A("idn"), A("icn")], [5])
-        ts(T.kn[:], kl, -1.0, OP.mult, [], [A("kn")], [4])
-        ts(T.nf[:], kl, 0.75, OP.is_lt, [], [A("nf")], [4])
-        ts(T.li[:], T.kn[:], 15, OP.bitwise_and, [A("kn")], [A("li")])
-        op("v", lambda e: e.tensor_tensor_scan(T.nfs[:, 1:17], T.nf[:], T.z16[:], 0.0, OP.add, OP.max), [A("nf"), A("z16")], [A("nfs")])
-        tt(T.lj[:], T.li[:], T.i16[:], OP.add, [A("li"), A("i16")], [A("lj")])
-        tt(T.nfi[:], T.nf[:], T.icr[:], OP.mult, [A("nf"), A("icr")], [A("nfi")])
-        cp(T.l16[:], T.lj[:], [A("lj")], [A("l16")])
-        mm(T.p5[:, 0:16], T.am[:], T.nf[:], False, False, [A("am"), A("nf")], [5])
-        mm(T.p5[:, 0:16], T.nbl[:], T.nfs[:, 0:16], False, False, [A("nbl"), A("nfs")], [5])
-        mm(T.p5[:, 0:16], T.idn[:], T.nfi[:], False, True, [A("idn"), A("nfi")], [5])
-        qw, qn = T["qw%d" % t], "qw%d" % t
-        cp(qw[:], T.qq[:].indirect(T.l16[:]), [A("qe"), A("qo"), A("l16")], [A(qn)])
-        for r in range(16):
-            mm(T.p1[:, 0:16], T.wu[:, 15 - r:143 - r], qw[:, r::16], r == 0, r == 15, [A("wu"), A(qn)], [1])
-        ts(T.ofi[:], T.p5[:, 0:16], 32.0, OP.mult, [], [A("ofi")], [5])
-        cp(T.uwi[:], T.p1[:, 0:16], [], [A("uwi")], [1])
-        ts(T.uwa[:], T.uwi[:], 31, OP.bitwise_and, [A("uwi")], [A("uwa")])
-        tt(T.tgi[:], T.uwa[:], T.ofi[:], OP.add, [A("uwa"), A("ofi")], [A("tgi")])
-        cp(T["tg%d" % t][:], T.tgi[:], [A("tgi")], [A("tg%d" % t)])
+    def send(t):
         dst = T.cores[(rank + 1 + t % (n_ranks - 1)) % n_ranks]
         es = topo.engines(core, dst)[:8]
         mask = sum(1 << e for e in es)
@@ -470,66 +332,221 @@ def rank_program(g, core, T, topo):
         src = T.cores[(rank - 1 - t % (n_ranks - 1)) % n_ranks]
         n_in = len(topo.engines(src, core)[:8])
         for a, b, sm in (("qw", "lq", "aq"), ("tg", "lt", "at")):
-            need("g", deps_of("g", [A("%s%d" % (a, t))], [], ()))
-            g.remote_dma(T["%s%d" % (b, t)][:], T["%s%d" % (a, t)][:], T.sem["%s%d" % (sm, t)], T.sem.ls, pid, rid, mask)
-            nloc[0] += len(es)
-            value[("%s%d" % (sm, t), 1)] = n_in
-            note(("%s%d" % (sm, t), 1), [], [A("%s%d" % (b, t))], ())
+            sn, dn, name = "%s%d" % (a, t), "%s%d" % (b, t), "%s%d" % (sm, t)
+            i = node("g", [lambda e, sn=sn, dn=dn, name=name: e.remote_dma(T[dn][:], T[sn][:], T.sem[name], T.sem.ls, pid, rid, mask)],
+                     1.0, [A(sn)], [], (), "r", len(es))
+            node(None, [], 0.0, [], [A(dn)], (), "a", (name, n_in), 2.5 if a == "qw" else 1.5, (i,))
+
+    def update(t, c):
+        ts(T.hf[:], T.hh[:], 16.0, OP.add, [A("hh")], [A("hf")], n=256)
+        for b in range(2):
+            mms([(T.p2[:, 128 * b:128 * b + 128], T.iv[:, 256 * par + 128 * b:256 * par + 128 * b + 128], T.hf[:, 128 * par:128 * par + 128],
+                  par == 0, par == 1) for par in range(2)], 512, [A("iv"), A("hf")], [2])
+        for H in range(2):
+            kt, sc, wn = T["kt%d" % H], T["sc%d" % H], T["wn%d" % H]
+            tt(wn[:], sc[:].indirect(T.cl[:]), kt[:], OP.is_equal, [A("kt%d" % H), A("cl"), A("sc%d" % H)], [A("wn%d" % H)], cost=0.25)
+            mms([(T.p2[:, 256 + 128 * H:384 + 128 * H], wn[:], T.idn[:], True, True)], 128, [A("wn%d" % H), A("idn")], [2])
+        E, M, S = A("ef%d" % c), A("mm%d" % c), A("sgn%d" % c)
+        for b in range(2):
+            d = T.de[:, 128 * b:128 * b + 128]
+            e = T.ef[:, c + 4 * b::8]
+            rg = ("de", b, b + 1)
+            tt(d, T.p2[:, 128 * b:128 * b + 128], e, OP.subtract, [E], [rg], [2], n=128)
+            tt(d, T.p2[:, 256 + b:512:2], d, OP.mult, [rg], [rg], [2], n=128)
+            tt(e, e, d, OP.add, [E, rg], [("ef%d" % c, b, b + 1)], n=256)
+        tt(T.tm[:], T.p2[:, 256:512], T.sgn[:, c::4], OP.mult, [S], [A("tm")], [2], n=256)
+        tt(T.mm[:, c::4], T.mm[:, c::4], T.tm[:], OP.add, [M, A("tm")], [M], n=512)
+
+    def out_lines(c):
+        act(T.ylb[:, c::4], T.ef[:, c::4], AF.Copy, [A("ef%d" % c)], [A("yl%d" % c)], n=256, bias=-16.0)
+
+    early_lists(0)
+    prep_x(0)
+    prep_s(0)
+    for c in range(1, 4):
+        early_lists(c)
+    win = T.xw[:, XC:XW]
+    WX = ("xw", XC, XW)
+    for t in range(RO):
+        c = t % 4
+        first = t == 0
+        gather_even(0)
+        gather_even(1)
+        gather_d(0)
+        gather_d(1)
+        hashes(0, 0, T.p0, 0, 0)
+        hashes(1, 0, T.p1, 64, 1)
+        hop(0, 64, T.p0[:, 0:64], 0, first)
+        hop(64, 128, T.p1[:, 64:128], 1, first)
+        scan(0)
+        odd_min(0)
+        hashes(0, 1, T.p1, 0, 1)
+        scan(1)
+        odd_min(1)
+        hashes(1, 1, T.p2, 0, 2)
+        hop(128, 192, T.p1[:, 0:64], 1, first)
+        hop(192, 256, T.p2[:, 0:64], 2, first)
+        for H, par in ((0, 0), (1, 0), (0, 1), (1, 1)):
+            look(H, par)
+        over(0)
+        gate(0)
+        over(1)
+        gate(1)
+        for H in range(2):
+            score(H, 0, c)
+            score(H, 1, c)
+            keys(H)
+        kl = T.p4[:, 0:16]
+        mms([(T.p5[:, 0:16], T.idn[:], T.icn[:], True, False)], 64, [A("idn"), A("icn")], [5])
+        ts(T.kn[:], kl, -1.0, OP.mult, [], [A("kn")], [4])
+        ts(T.nf[:], kl, 0.75, OP.is_lt, [], [A("nf")], [4])
+        ts(T.li[:], T.kn[:], 15, OP.bitwise_and, [A("kn")], [A("li")])
+        tt(T.lj[:], T.li[:], T.i16[:], OP.add, [A("li"), A("i16")], [A("lj")])
+        cp(T.l16[:], T.lj[:], [A("lj")], [A("l16")])
+        qw, qn = T["qw%d" % t], "qw%d" % t
+        cp(qw[:], T.qq[:].indirect(T.l16[:]), [A("qe"), A("qo"), A("l16")], [A(qn)], cost=0.05 + 256 * GAT)
+        mms([(T.p1[:, 0:16], T.wu[:, 15 - r:143 - r], qw[:, r::16], r == 0, r == 15) for r in range(16)], 64, [A("wu"), A(qn)], [1])
+        scn(T.nfs[:, 1:17], T.nf[:], T.z16[:], 0.0, OP.add, OP.max, [A("nf"), A("z16")], [A("nfs")], 16)
+        tt(T.nfi[:], T.nf[:], T.icr[:], OP.mult, [A("nf"), A("icr")], [A("nfi")])
+        mms([(T.p5[:, 0:16], T.am[:], T.nf[:], False, False), (T.p5[:, 0:16], T.nbl[:], T.nfs[:, 0:16], False, False),
+             (T.p5[:, 0:16], T.idn[:], T.nfi[:], False, True)], 64, [A("am"), A("nf"), A("nbl"), A("nfs"), A("idn"), A("nfi")], [5])
+        ts(T.ofi[:], T.p5[:, 0:16], 32.0, OP.mult, [], [A("ofi")], [5])
+        cp(T.uwi[:], T.p1[:, 0:16], [], [A("uwi")], [1])
+        ts(T.uwa[:], T.uwi[:], 31, OP.bitwise_and, [A("uwi")], [A("uwa")])
+        tt(T.tgi[:], T.uwa[:], T.ofi[:], OP.add, [A("uwa"), A("ofi")], [A("tgi")])
+        cp(T["tg%d" % t][:], T.tgi[:], [A("tgi")], [A("tg%d" % t)])
+        send(t)
+        if t == 3:
+            update(t, c)
         if t < RO - 1:
-            mm(T.p5[:, 32:48], T.one[:], T.nf[:], True, True, [A("one"), A("nf")], [5])
-            op("v", lambda e: e.tensor_reduce(T.kc[:], T.p5[:, 32:48], AxisListType.X, OP.add), [], [A("kc")], [5])
+            if t < 3:
+                prep_x(t + 1)
+                prep_s(t + 1)
+            else:
+                prep_x(0)
+                prep_s(0)
+            mms([(T.p5[:, 32:48], T.one[:], T.nf[:], True, True)], 64, [A("one"), A("nf")], [5])
+            node("v", [lambda e: e.tensor_reduce(T.kc[:], T.p5[:, 32:48], AxisListType.X, OP.add)], cy(16), [], [A("kc")], [5])
             ts(T.kci[:], T.kc[:], -1.0, OP.mult, [A("kc")], [A("kci")])
             ts(T.kcj[:], T.kci[:], 31, OP.bitwise_and, [A("kci")], [A("kcj")])
             cp(T.kap[:], T.kcj[:], [A("kcj")], [A("kap")])
-            if t < 3:
-                early_lists(t + 1)
-                prep_x((t + 1) % 4)
-                prep_s((t + 1) % 4)
-                ts(T.ek[:], T.ei[:], T.kap[:], OP.add, [A("ei"), A("kap")], [A("ek")])
-
-        def update():
-            ts(T.hf[:], T.hh[:], 16.0, OP.add, [A("hh")], [A("hf")])
-            for b in range(2):
-                for par in range(2):
-                    j = 2 * par + b
-                    mm(T.p2[:, 128 * b:128 * b + 128], T.iv[:, 128 * j:128 * j + 128], T.hf[:, 128 * par:128 * par + 128], par == 0, par == 1,
-                       [A("iv"), A("hf")], [2])
-            for H in range(2):
-                kt, sc, wn = T["kt%d" % H], T["sc%d" % H], T["wn%d" % H]
-                tt(wn[:], sc[:].indirect(T.cl[:]), kt[:], OP.is_equal, [A("kt%d" % H), A("cl"), A("sc%d" % H)], [A("wn%d" % H)])
-                mm(T.p5[:, 128 + 128 * H:256 + 128 * H], wn[:], T.idn[:], True, True, [A("wn%d" % H), A("idn")], [5])
-            R = A("ef%d" % c)
-            for b in range(2):
-                d = T.de[:, 128 * b:128 * b + 128]
-                e = T.ef[:, c + 4 * b::8]
-                rg = ("de", b, b + 1)
-                tt(d, T.p2[:, 128 * b:128 * b + 128], e, OP.subtract, [R], [rg], [2])
-                tt(d, T.p5[:, 128 + b:384:2], d, OP.mult, [rg], [rg], [5])
-                tt(e, e, d, OP.add, [R, rg], [("ef%d" % c, b, b + 1)])
-            tt(T.tm[:], T.p5[:, 128:384], T.sgn[:, c::4], OP.mult, [A("sgn")], [A("tm")], [5])
-            tt(T.mm[:, c::4], T.mm[:, c::4], T.tm[:], OP.add, [A("mm"), A("tm")], [A("mm")])
-        if t < 3:
-            update()
-        elif t == 3:
-            prep_x(0)
-            prep_s(0)
-            ts(T.ek[:], T.ei[:], T.kap[:], OP.add, [A("ei"), A("kap")], [A("ek")])
-            update()
-        else:
-            update()
-            dma("y", T.ym[:], T.mm[:], [A("mm")], [])
-            ts(T.ylb[:], T.ef[:], -16.0, OP.add, [A("ef0"), A("ef1"), A("ef2"), A("ef3")], [A("ylb")])
-            dma("s", T.yl[:], T.ylb[:], [A("ylb")], [])
-        win = T.xw[:, XC:XW]
-        WX = ("xw", XC, XW)
+            ts(T.ek[:], T.ei[:], T.kap[:], OP.add, [A("ei"), A("kap")], [A("ek")], n=256)
+        if t != 3:
+            update(t, c)
+        if t > 0:
+            out_lines(c)
         lt = T["lt%d" % t]
-        tt(T.av[:], win.indirect(lt[:]), T["lq%d" % t][:], OP.add, [WX, A("lt%d" % t), A("lq%d" % t)], [A("av")])
-        ts(T.ai[:], T.av[:], 0.5, OP.mult, [A("av")], [A("ai")], (), -0.25, OP.add)
-        cp(win.indirect(lt[:]), T.ai[:], [A("ai"), A("lt%d" % t)], [WX])
-    dma("y", T.yx[:, 0:2048], T.xw[:, XC:XC + 2048], [WX], [])
-    dma("s", T.yx[:, 2048:4096], T.xw[:, XC + 2048:XC + 4096], [WX], [])
+        L = A("lt%d" % t)
+        tt(T.av[:], win.indirect(lt[:]), T["lq%d" % t][:], OP.add, [WX, L, A("lq%d" % t)], [A("av")], cost=0.05 + 256 * GAT)
+        ts(T.ai[:], T.av[:], 0.5, OP.mult, [A("av")], [A("ai")], (), -0.25, OP.add, n=256)
+        cp(win.indirect(lt[:]), T.ai[:], [A("ai"), L], [WX], cost=0.05 + 256 * SCA)
+    dma("y", T.ym[:], T.mm[:], MM4, [], 262144)
+    dma("s", T.yl[:], T.ylb[:], [A("yl%d" % c) for c in range(4)], [], 524288)
+    dma("y", T.yx[:, 0:2048], T.xw[:, XC:XC + 2048], [WX], [], 1048576)
+    dma("s", T.yx[:, 2048:4096], T.xw[:, XC + 2048:XC + 4096], [WX], [], 1048576)
+
+    n = len(nodes)
+    before = [[] for _ in range(n)]
+    after = [[] for _ in range(n)]
+    for i, d in enumerate(nodes):
+        for j in d["deps"] | d["order"]:
+            f = nodes[j]
+            lag = f["late"] + ((0.03 if f["q"] == d["q"] else 0.1) if j in d["deps"] else 0.0)
+            before[i].append((j, lag))
+            after[j].append((i, lag))
+
+    def arrange(pre, post, prio):
+        left = [len(x) for x in pre]
+        end = [0.0] * n
+        free = {q: 0.0 for q in eng}
+        ready = {q: [] for q in eng}
+        out, todo = [], [i for i in range(n) if not pre[i]]
+        first = True
+        while True:
+            while todo:
+                i = todo.pop()
+                rel = [i] if first and not pre[i] else []
+                if not rel:
+                    for j, _ in post[i]:
+                        left[j] -= 1
+                        if left[j] == 0:
+                            rel.append(j)
+                for j in rel:
+                    r = max([end[k] + lag for k, lag in pre[j]] + [0.0])
+                    if nodes[j]["q"] is None:
+                        end[j] = r
+                        out.append(j)
+                        todo.append(j)
+                    else:
+                        ready[nodes[j]["q"]].append((r, j))
+            first = False
+            best = None
+            for q in eng:
+                if ready[q]:
+                    s0 = min(max(free[q], r) for r, _ in ready[q])
+                    if best is None or s0 < best[0]:
+                        best = (s0, q)
+            if best is None:
+                return out, end
+            s0, q = best
+            pick = max((x for x in ready[q] if max(free[q], x[0]) <= s0 + 0.06), key=lambda x: (prio[x[1]], -x[1]))
+            ready[q].remove(pick)
+            i = pick[1]
+            free[q] = end[i] = max(free[q], pick[0]) + nodes[i]["cost"]
+            out.append(i)
+            todo.append(i)
+    prio = [0.0] * n
+    for i in range(n - 1, -1, -1):
+        prio[i] = nodes[i]["cost"] + max([prio[j] + lag for j, lag in after[i]] + [0.0])
+    best = None
+    for _ in range(PASSES):
+        out, end = arrange(before, after, prio)
+        if best is None or max(end) < best[0]:
+            best = (max(end), out, end)
+        _, prio = arrange(after, before, end)
+    orders, fin = best[1], best[2]
+
+    cnt = {q: 0 for q in eng}
+    known = {q: {} for q in eng}
+    stamp, snap = {}, {}
+    nloc = 0
+    for i in orders:
+        d = nodes[i]
+        q = d["q"]
+        if q is None:
+            stamp[i] = (d["key"][0], 1, d["key"][1])
+            snap[i] = {}
+            continue
+        kq = known[q]
+        latest = {}
+        for j in d["deps"]:
+            s, k, v = stamp[j]
+            if s not in latest or latest[s][0] < k:
+                latest[s] = (k, v, j)
+        for s in sorted(latest, key=lambda s: -fin[latest[s][2]]):
+            k, v, j = latest[s]
+            if kq.get(s, 0) >= k:
+                continue
+            eng[q].wait_ge(T.sem[s], v)
+            kq[s] = k
+            for s2, k2 in snap[j].items():
+                if k2 > kq.get(s2, 0):
+                    kq[s2] = k2
+        snap[i] = dict(kq)
+        if d["kind"] == "d":
+            d["calls"][0](eng[q]).then_inc(T.sem[d["key"]], 16)
+            stamp[i] = (d["key"], 1, 16)
+        elif d["kind"] == "r":
+            d["calls"][0](eng[q])
+            nloc += d["key"]
+            stamp[i] = ("ls", nloc, nloc)
+        else:
+            for f in d["calls"]:
+                f(eng[q]).then_inc(T.sem[semname[q]], 1)
+                cnt[q] += 1
+            stamp[i] = (semname[q], cnt[q], cnt[q])
     for q in ("v", "s", "p", "g"):
         g.wait_ge(T.sem[semname[q]], cnt[q])
     for j in range(ndma[0]):
         g.wait_ge(T.sem["dm%d" % j], 16)
-    g.wait_ge(T.sem.ls, nloc[0])
+    g.wait_ge(T.sem.ls, nloc)

from concourse.bass import DstId, RemoteDMATransfer
from concourse.mybir import dt, AluOpType, AxisListType, ActivationFunctionType

OP = AluOpType
AF = ActivationFunctionType
RO = 5
XC = 16
XW = XC + 512 * 32
LOOK_S = ((0, 0), (0, 1))
EVEN_V = (0, 1)

SCRATCH = {"xw": ("sbuf", [128, XW], "bfloat16"), "alt": ("sbuf", [128, 2048], "bfloat16")}
for _n, _w, _d in (
        ("ei0", 1024, "int32"), ("ef", 1024, "float32"), ("mm", 1024, "bfloat16"), ("sgn", 1024, "bfloat16"), ("ylb", 1024, "float32"),
        ("d0", 4096, "bfloat16"), ("bb", 4096, "bfloat16"), ("qq", 4096, "bfloat16"), ("dq", 4096, "bfloat16"), ("sg", 4096, "bfloat16"),
        ("ov", 4096, "bfloat16"), ("yb", 4096, "bfloat16"),
        ("dl16", 256, "uint16"), ("el16", 256, "uint16"), ("h16", 256, "uint16"), ("ei", 256, "int32"), ("ek", 256, "int32"),
        ("ui", 256, "int32"), ("ua", 256, "int32"), ("ta", 256, "int32"), ("tb", 256, "int32"), ("tc", 256, "int32"), ("hh", 256, "int32"),
        ("hf", 256, "float32"), ("de", 256, "float32"), ("td", 256, "float32"), ("tm", 256, "bfloat16"), ("av", 256, "float32"), ("ai", 256, "int32"),
        ("pi", 1, "int32"), ("ci", 8, "int32"), ("cf", 32, "float32"), ("m1", 160, "float32"), ("si", 128, "float32"), ("clf", 8, "float32"),
        ("cl", 8, "uint16"), ("icf", 16, "float32"), ("icn", 16, "bfloat16"), ("icr", 16, "bfloat16"), ("i16", 16, "int32"), ("mg", 128, "float32"),
        ("idn", 128, "bfloat16"), ("nid", 128, "bfloat16"), ("nk", 128, "bfloat16"), ("g8", 8, "bfloat16"), ("rcp", 8, "bfloat16"),
        ("wu", 144, "bfloat16"), ("pm", 512, "float32"), ("iv", 512, "float32"), ("nbl", 128, "bfloat16"), ("lt", 128, "bfloat16"),
        ("idx", 128, "bfloat16"), ("t1", 128, "bfloat16"), ("am", 128, "bfloat16"), ("one", 128, "bfloat16"), ("mr", 128, "bfloat16"),
        ("ke", 128, "bfloat16"), ("z16", 16, "bfloat16"),
        ("ge", 256, "bfloat16"), ("gsg", 256, "bfloat16"), ("sgt", 256, "bfloat16"), ("kt0", 128, "bfloat16"), ("kt1", 128, "bfloat16"),
        ("sc0", 128, "bfloat16"), ("sc1", 128, "bfloat16"), ("lm0", 128, "bfloat16"), ("lm1", 128, "bfloat16"), ("wn0", 128, "bfloat16"),
        ("wn1", 128, "bfloat16"), ("nf", 16, "bfloat16"), ("nfs", 32, "bfloat16"), ("nfi", 16, "bfloat16"), ("kn", 16, "int32"), ("li", 16, "int32"),
        ("lj", 16, "int32"), ("l16", 16, "uint16"), ("ofi", 16, "int32"), ("uwi", 16, "int32"), ("uwa", 16, "int32"), ("tgi", 16, "int32"),
        ("kc", 1, "float32"), ("kci", 1, "int32"), ("kcj", 1, "int32"), ("kap", 1, "float32")):
    SCRATCH[_n] = ("sbuf", [128, _w], _d)
for _t in range(8):
    SCRATCH["p%d" % _t] = ("psum", [128, 512], "float32")
for _t in range(RO):
    SCRATCH["qw%d" % _t] = ("sbuf", [128, 256], "bfloat16")
    SCRATCH["lq%d" % _t] = ("sbuf", [128, 256], "bfloat16")
    SCRATCH["tg%d" % _t] = ("sbuf", [128, 16], "uint16")
    SCRATCH["lt%d" % _t] = ("sbuf", [128, 16], "uint16")
SEMAPHORES = ["cv", "cs", "cp", "cg", "ls"] + ["aq%d" % _t for _t in range(RO)] + ["at%d" % _t for _t in range(RO)] \
    + ["dm%d" % _t for _t in range(24)]

PASSES = 12
CYC = 0.001
GAT = 0.00150
SCA = 0.0030


def rank_program(g, core, T, topo):
    rank = T.rank_of(core)
    if rank is None:
        return
    n_ranks = len(T.cores)
    eng = {"v": g.vector, "s": g.scalar, "p": g.tensor, "g": g, "y": g.sync}
    semname = {"v": "cv", "s": "cs", "p": "cp", "g": "cg"}

    nodes = []
    wr, rd, bank = {}, {}, {}
    ndma = [0]

    def node(q, calls, cost, R, W, B=(), kind="c", key=None, late=0.0, extra=()):
        d = set(extra)
        for (b, lo, hi) in R:
            for (l, h, i) in wr.get(b, ()):
                if l < hi and lo < h:
                    d.add(i)
        for (b, lo, hi) in W:
            for (l, h, i) in wr.get(b, ()):
                if l < hi and lo < h:
                    d.add(i)
            for (l, h, i) in rd.get(b, ()):
                if l < hi and lo < h:
                    d.add(i)
        me = len(nodes)
        order = set()
        for b in B:
            if b in bank:
                (order if nodes[bank[b]]["q"] == q else d).add(bank[b])
                for j in nodes[bank[b]]["chain"].get(b, ()):
                    if nodes[j]["q"] != q:
                        d.add(j)
        chain = {}
        for b in B:
            last = {}
            if b in bank:
                for j in nodes[bank[b]]["chain"].get(b, ()):
                    last[nodes[j]["q"]] = j
                last[nodes[bank[b]]["q"]] = bank[b]
            chain[b] = list(last.values())
        nodes.append({"q": q, "calls": calls, "cost": cost, "deps": d, "order": order - d, "kind": kind, "key": key, "late": late, "chain": chain})
        for b in B:
            bank[b] = me
        for (b, lo, hi) in W:
            wr[b] = [e for e in wr.get(b, ()) if not (lo <= e[0] and e[1] <= hi)] + [(lo, hi, me)]
            rd[b] = [e for e in rd.get(b, ()) if not (lo <= e[0] and e[1] <= hi)]
        for (b, lo, hi) in R:
            rd.setdefault(b, []).append((lo, hi, me))
        return me

    def dma(q, out, in_, R, W, by):
        name = "dm%d" % ndma[0]
        ndma[0] += 1
        node(q, [lambda e: e.dma_start(out, in_)], 0.1, R, W, (), "d", name, 2.0 + by * 4e-6)

    def A(b, lo=0, hi=1 << 20):
        return (b, lo, hi)

    def cy(n):
        return max(64, n) * CYC

    def mms(lst, n, R, B):
        node("p", [lambda e, a=a: e.matmul(*a) for a in lst], len(lst) * n * CYC, R, [], B)

    def ts(out, in0, s1, o1, R, W, B=(), s2=None, o2=None, n=64):
        if o2 is None:
            node("v", [lambda e: e.tensor_scalar(out, in0, s1, None, o1)], cy(n), R, W, B)
        else:
            node("v", [lambda e: e.tensor_scalar(out, in0, s1, s2, o1, o2)], cy(n), R, W, B)

    def tt(out, a, b, o, R, W, B=(), n=64, cost=None):
        node("v", [lambda e: e.tensor_tensor(out, a, b, o)], cost or cy(n), R, W, B)

    def cp(out, in_, R, W, B=(), n=64, cost=None):
        node("v", [lambda e: e.tensor_copy(out, in_)], cost or cy(n), R, W, B)

    def scn(out, a, b, init, o1, o2, R, W, n):
        node("v", [lambda e: e.tensor_tensor_scan(out, a, b, init, o1, o2)], cy(n), R, W)

    def act(out, in_, f, R, W, B=(), n=64, cost=None, **kw):
        node("s", [lambda e: e.activation(out, in_, f, **kw)], cost or cy(n), R, W, B)

    def fill(ap, c, W, n=64):
        node("v", [lambda e: e.memset(ap, c)], cy(n), [], W)

    def iota(ap, pat, base, cm, W, n, fl=True):
        if fl:
            node("g", [lambda e: e.iota(ap, pat, base, cm, allow_small_or_imprecise_dtypes=True)], 0.13 + 2 * n * CYC, [], W)
        else:
            node("g", [lambda e: e.iota(ap, pat, base, cm)], 0.13 + 2 * n * CYC, [], W)

    MM4 = [A("mm%d" % c) for c in range(4)]
    dma("y", T.ei0[:], T.led[:], [], [A("ei0")], 524288)
    dma("s", T.mm[:], T.mk[:], [], MM4, 262144)
    dma("y", T.xw[:, XC:XC + 2048], T.xt[:, 0:2048], [], [A("xw", XC, XC + 2048)], 1048576)
    dma("s", T.xw[:, XC + 2048:XC + 4096], T.xt[:, 2048:4096], [], [A("xw", XC + 2048, XC + 4096)], 1048576)
    dma("y", T.xw[:, XC + 4096:XC + 8192], T.xt[:], [], [A("xw", XC + 4096, XC + 8192)], 2500000)
    dma("s", T.xw[:, XC + 8192:XC + 12288], T.xt[:], [], [A("xw", XC + 8192, XC + 12288)], 2500000)

    iota(T.pi[:], [[0, 1]], 0, 1, [A("pi")], 1, False)
    iota(T.m1[:], [[1, 160]], 1, 0, [A("m1")], 160)
    iota(T.clf[:], [[16, 8]], 15, 0, [A("clf")], 8)
    iota(T.mg[:], [[16, 8], [0, 16]], 0, 0, [A("mg")], 128)
    iota(T.si[:], [[0, 8], [1, 16]], 0, 0, [A("si")], 128)
    iota(T.icf[:], [[16, 16]], 0, 1, [A("icf")], 16)
    fill(T.xw[:, 0:16], 0.0, [A("xw", 0, 16)])
    fill(T.xw[:, 1:2], 4096.0, [A("xw", 0, 16)])
    fill(T.alt[:, 0::2], 4096.0, [A("alt", 0, 1)], 512)
    fill(T.alt[:, 1::2], 0.0, [A("alt", 1, 2)], 512)

    def ci(j):
        return T.ci[:, j:j + 1]

    def cf(j):
        return T.cf[:, j:j + 1]

    def rc(j):
        return ("cf", j, j + 1)
    ts(ci(0), T.pi[:], 15, OP.bitwise_and, [A("pi")], [("ci", 0, 1)])
    ts(ci(1), T.pi[:], 3, OP.logical_shift_right, [A("pi")], [("ci", 1, 2)], (), 1, OP.bitwise_and)
    ts(ci(2), T.pi[:], 1, OP.bitwise_and, [A("pi")], [("ci", 2, 3)])
    ts(ci(3), T.pi[:], 1, OP.logical_shift_right, [A("pi")], [("ci", 3, 4)], (), 7, OP.bitwise_and)
    ts(ci(4), T.pi[:], 7, OP.bitwise_and, [A("pi")], [("ci", 4, 5)])
    cp(T.cf[:, 0:5], T.ci[:, 0:5], [("ci", 0, 5)], [("cf", 0, 5)])
    cp(cf(5), T.pi[:], [A("pi")], [rc(5)])
    tt(cf(6), cf(5), cf(0), OP.subtract, [rc(5), rc(0)], [rc(6)])
    ts(cf(7), cf(2), -1.0, OP.mult, [rc(2)], [rc(7)], (), 1.0, OP.add)
    ts(cf(8), cf(1), -1.0, OP.mult, [rc(1)], [rc(8)], (), 1.0, OP.add)
    tt(cf(9), cf(6), cf(3), OP.add, [rc(6), rc(3)], [rc(9)])
    ts(cf(10), cf(4), 2.0, OP.mult, [rc(4), rc(6)], [rc(10)], (), cf(6), OP.add)
    for par in range(2):
        for b in range(2):
            j = 11 + 2 * par + b
            ts(cf(j), cf(9), float(8 * b + 1), OP.add, [rc(9), rc(7), rc(2)], [rc(j)], (), cf(2 if par else 7), OP.mult)
            j = 15 + 2 * par + b
            ts(cf(j), cf(10), float(par + 1), OP.add, [rc(10), rc(1), rc(8)], [rc(j)], (), cf(1 if b else 8), OP.mult)
    for j in range(4):
        ts(T.pm[:, 128 * j:128 * j + 128], T.m1[:, 0:128], cf(11 + j), OP.is_equal, [A("m1"), rc(11 + j)], [("pm", j, j + 1)], n=128)
        ts(T.iv[:, 128 * j:128 * j + 128], T.m1[:, 0:128], cf(15 + j), OP.is_equal, [A("m1"), rc(15 + j)], [("iv", j, j + 1)], n=128)
    ts(cf(19), cf(0), 14.5, OP.is_lt, [rc(0)], [rc(19)])
    ts(cf(20), cf(0), 14.5, OP.is_gt, [rc(0)], [rc(20)])
    ts(cf(21), cf(0), 2.0, OP.mult, [rc(0)], [rc(21)], (), 1.0, OP.add)
    ts(cf(22), cf(6), 16.0, OP.add, [rc(6)], [rc(22)])
    ts(cf(23), cf(0), -1.0, OP.mult, [rc(0)], [rc(23)])
    ts(cf(25), cf(6), 0.0625, OP.mult, [rc(6)], [rc(25)], (), 1.0, OP.add)
    ts(cf(26), cf(5), 1.0, OP.add, [rc(5)], [rc(26)])
    ts(T.wu[:], T.m1[:, 0:144], cf(22), OP.is_equal, [A("m1"), rc(22), rc(21)], [A("wu")], (), cf(21), OP.mult, n=144)
    ts(T.idn[:], T.m1[:, 0:128], cf(26), OP.is_equal, [A("m1"), rc(26)], [A("idn")], n=128)
    ts(T.nid[:], T.m1[:, 0:128], cf(26), OP.is_equal, [A("m1"), rc(26)], [A("nid")], (), -1.0, OP.mult, n=128)
    ts(T.idx[:], T.m1[:, 0:128], cf(26), OP.is_equal, [A("m1"), rc(26)], [A("idx")], (), 256.0, OP.mult, n=128)
    ts(T.nk[:], T.m1[:, 0:128], cf(26), OP.is_equal, [A("m1"), rc(26), rc(23)], [A("nk")], (), cf(23), OP.mult, n=128)
    ts(T.g8[:], T.m1[:, 0:8], cf(25), OP.is_equal, [A("m1"), rc(25)], [A("g8")], (), 16.0, OP.mult)
    ts(T.rcp[:], T.m1[:, 0:8], cf(25), OP.is_equal, [A("m1"), rc(25)], [A("rcp")])
    ts(T.nbl[:], T.mg[:], cf(6), OP.is_equal, [A("mg"), rc(6)], [A("nbl")], (), -1.0, OP.mult, n=128)
    ts(T.lt[:], T.m1[:, 0:128], cf(26), OP.is_gt, [A("m1"), rc(26)], [A("lt")], n=128)
    tt(T.t1[:], T.nbl[:], T.lt[:], OP.mult, [A("nbl"), A("lt")], [A("t1")], n=256)
    tt(T.am[:], T.idx[:], T.t1[:], OP.add, [A("idx"), A("t1")], [A("am")], n=256)
    ts(T.icf[:], T.icf[:], cf(6), OP.subtract, [A("icf"), rc(6)], [A("icf")])
    cp(T.icn[:], T.icf[:], [A("icf")], [A("icn")])
    ts(T.icr[:], T.icf[:], -1.0, OP.mult, [A("icf")], [A("icr")], (), 255.0, OP.add)
    ts(T.i16[:], T.icf[:], 16.0, OP.mult, [A("icf")], [A("i16")])
    ts(T.mr[:], T.si[:], cf(0), OP.is_equal, [A("si"), rc(0)], [A("mr")], n=128)
    cp(T.cl[:], T.clf[:], [A("clf")], [A("cl")])
    fill(T.ke[:], 512.0, [A("ke")])
    fill(T.ke[:, 0::16], 0.5, [A("ke")])
    fill(T.z16[:], 0.0, [A("z16")])
    fill(T.nfs[:], 0.0, [A("nfs")])
    fill(T.one[:], 1.0, [A("one")])
    for z in range(4):
        lo = XC + 12288 + 1024 * z
        fill(T.xw[:, lo:lo + 1024], 0.0, [A("xw", lo, lo + 1024)], 512)

    def early_lists(c):
        ts(T.ef[:, c::4], T.ei0[:, c::4], 16.0, OP.add, [A("ei0")], [A("ef%d" % c)], n=256)

    def prep_x(c):
        E, M = A("ef%d" % c), A("mm%d" % c)
        tt(T.td[:], T.ef[:, c::4], T.mm[:, c::4], OP.mult, [E, M], [A("td")], n=512)
        ts(T.dl16[:], T.td[:], cf(19), OP.mult, [A("td"), rc(19), rc(20)], [A("dl16")], (), cf(20), OP.add, n=256)
        for par in range(2):
            mms([(T.p0[:, 128 * par:128 * par + 128], T.pm[:, 256 * par + 128 * b:256 * par + 128 * b + 128], T.ef[:, c + 4 * b::8], b == 0, b == 1)
                 for b in range(2)], 512, [A("pm"), E], [0])
        cp(T.el16[:], T.p0[:, 0:256], [], [A("el16")], [0], n=256)
        ts(T.ei[:], T.p0[:, 0:256], -16.0, OP.add, [], [A("ei")], [0], n=256)

    def prep_s(c):
        act(T.sgn[:, c::4], T.mm[:, c::4], AF.Copy, [A("mm%d" % c)], [A("sgn%d" % c)], n=256, scale=-2.0, bias=1.0)
        mms([(T.p3[:, 256 + 128 * H:384 + 128 * H], T.sgn[:, 512 * H + c:512 * H + 512:4], T.idn[:], True, True) for H in range(2)],
            128, [A("sgn%d" % c), A("idn")], [3])
        act(T.sgt[:], T.p3[:, 256:512], AF.Copy, [], [A("sgt")], [3], n=256)

    items = T.xw[:, XC:XC + 4096]
    all_x = T.xw[:, 0:XC + 4096]
    RX = ("xw", 0, XC + 4096)

    def gather_even(H):
        out = T.qq[:, 2048 * H:2048 * H + 2048:2]
        src = all_x.indirect(T.el16[:, 64 * H:64 * H + 64])
        f = cp if H in EVEN_V else (lambda o, i, R, W, cost: act(o, i, AF.Copy, R, W, cost=cost))
        f(out, src, [RX, A("el16")], [("qe", H, H + 1)], cost=0.06 + 1024 * GAT)

    def gather_d(H):
        act(T.d0[:, 2048 * H:2048 * H + 2048], all_x.indirect(T.dl16[:, 128 * H:128 * H + 128]), AF.Copy,
            [RX, A("dl16")], [("d0", H, H + 1)], cost=0.06 + 2048 * GAT)

    def hashes(H, par, ps, col, B):
        mms([(ps[:, col:col + 64], T.wu[:, 15 - r:143 - r], T.qq[:, 2048 * H + 2 * r + par:2048 * H + 2048:32], r == 0, r == 15) for r in range(16)],
            64, [A("wu"), ("qo" if par else "qe", H, H + 1)], [B])

    def hop(lo, hi, src, B, first):
        s = slice(lo, hi)
        n = hi - lo

        def rg(b):
            return (b, lo, hi)
        cp(T.ui[:, s], src, [], [rg("ui")], [B], n=n)
        ts(T.ua[:, s], T.ui[:, s], 4095, OP.bitwise_and, [rg("ui")], [rg("ua")], n=n)
        tt(T.ta[:, s], T.ei[:, s], T.ua[:, s], OP.mult, [A("ei"), rg("ua")], [rg("ta")], n=2 * n)
        ts(T.tb[:, s], T.ta[:, s], 5, OP.logical_shift_right, [rg("ta")], [rg("tb")], n=n)
        e, en = (T.ei, "ei") if first else (T.ek, "ek")
        tt(T.tc[:, s], T.tb[:, s], e[:, s], OP.add, [rg("tb"), A(en)], [rg("tc")], n=2 * n)
        ts(T.hh[:, s], T.tc[:, s], 4095, OP.bitwise_and, [rg("tc")], [rg("hh")], n=n)
        cp(T.h16[:, s], T.hh[:, s], [rg("hh")], [rg("h16")], n=n)

    def scan(H):
        s = slice(2048 * H, 2048 * H + 2048)
        scn(T.bb[:, s], T.d0[:, s], T.alt[:], 0.0, OP.subtract, OP.min, [("d0", H, H + 1), A("alt")], [("bb", H, H + 1)], 1024)

    def odd_min(H):
        tt(T.qq[:, 2048 * H + 1:2048 * H + 2048:2], all_x.indirect(T.el16[:, 128 + 64 * H:192 + 64 * H]),
           T.bb[:, 2048 * H:2048 * H + 2048:2], OP.min, [RX, A("el16"), ("bb", H, H + 1)], [("qo", H, H + 1)], cost=0.06 + 1024 * GAT)

    def look(H, par):
        s = slice(2048 * H + par, 2048 * H + 2048, 2)
        lo = 128 * par + 64 * H
        z = 2 * H + par
        Q = ("qo" if par else "qe", H, H + 1)
        if (H, par) in LOOK_S:
            act(T.yb[:, 1024 * z:1024 * z + 1024], items.indirect(T.h16[:, lo:lo + 64]), AF.Copy, [RX, ("h16", lo, lo + 64)], [("yb", z, z + 1)],
                cost=0.07 + 1024 * GAT)
            for x in range(2):
                ps, B = (T.p5, 5) if x else (T.p4, 4)
                qs = slice(2048 * H + par + 1024 * x, 2048 * H + 1024 * x + 1024, 2)
                mms([(ps[:], T.idn[:], T.yb[:, 1024 * z + 512 * x:1024 * z + 512 * x + 512], True, False),
                     (ps[:], T.nid[:], T.qq[:, qs], False, True)], 512, [A("idn"), A("nid"), ("yb", z, z + 1), Q], [B])
                act(T.sg[:, qs], ps[:], AF.Sign, [], [("sg", 4 * H + 2 * par + x, 4 * H + 2 * par + x + 1)], [B], n=512)
            return
        tt(T.dq[:, s], items.indirect(T.h16[:, lo:lo + 64]), T.qq[:, s], OP.subtract,
           [RX, ("h16", lo, lo + 64), Q], [("dq", z, z + 1)], cost=0.06 + 1024 * GAT)
        ts(T.sg[:, s], T.dq[:, s], 1.0, OP.min, [("dq", z, z + 1)], [("sg", 2 * z, 2 * z + 2)], (), -1.0, OP.max, n=512)

    def score(H, par, c):
        ps, B = (T.p7, 7) if H else (T.p6, 6)
        if par == 0:
            mms([(ps[:, 0:128], T.sgn[:, 512 * H + c:512 * H + 512:4], T.nk[:], True, False)], 128, [A("sgn%d" % c), A("nk")], [B])
        z = 2 * H + par
        mms([(ps[:, k:128:16], T.sg[:, 2048 * H + k:2048 * H + 2048:16], T.g8[:], False, k == 15) for k in range(par, 16, 2)],
            64, [("sg", 2 * z, 2 * z + 2), A("g8")], [B])

    def over(H):
        act(T.ov[:, 2048 * H:2048 * H + 2048], T.qq[:, 2048 * H:2048 * H + 2048], AF.Sign,
            [("qe", H, H + 1), ("qo", H, H + 1)], [("ov", H, H + 1)], n=2048)
        mms([(T.p3[:, 128 * H + k:128 * H + 128:16], T.ov[:, 2048 * H + k:2048 * H + 2048:16], T.g8[:], True, True) for k in range(16)],
            64, [("ov", H, H + 1), A("g8")], [3])

    def gate(H):
        s = slice(128 * H, 128 * H + 128)
        ts(T.ge[:, s], T.p3[:, s], 136.0, OP.is_gt, [], [("ge", H, H + 1)], [3], n=128)
        tt(T.gsg[:, s], T.ge[:, s], T.sgt[:, s], OP.mult, [("ge", H, H + 1), A("sgt")], [("gsg", H, H + 1)], n=256)

    def keys(H):
        ps, B = (T.p7, 7) if H else (T.p6, 6)
        kt, sc, lm = T["kt%d" % H], T["sc%d" % H], T["lm%d" % H]
        tt(kt[:], ps[:, 0:128], T.gsg[:, 128 * H:128 * H + 128], OP.mult, [("gsg", H, H + 1)], [A("kt%d" % H)], [B], n=128)
        scn(sc[:], T.ke[:], kt[:], 0.5, OP.min, OP.max, [A("ke"), A("kt%d" % H)], [A("sc%d" % H)], 64)
        tt(lm[:], sc[:].indirect(T.cl[:]), T.mr[:], OP.mult, [A("sc%d" % H), A("cl"), A("mr")], [A("lm%d" % H)], cost=0.25)
        mms([(T.p4[:, 8 * H:8 * H + 8], lm[:], T.rcp[:], True, True)], 64, [A("lm%d" % H), A("rcp")], [4])

    def send(t):
        dst = T.cores[(rank + 1 + t % (n_ranks - 1)) % n_ranks]
        es = topo.engines(core, dst)[:8]
        mask = sum(1 << e for e in es)
        rid, pid, _ = topo.addr(dst)
        src = T.cores[(rank - 1 - t % (n_ranks - 1)) % n_ranks]
        n_in = len(topo.engines(src, core)[:8])
        for a, b, sm in (("qw", "lq", "aq"), ("tg", "lt", "at")):
            sn, dn, name = "%s%d" % (a, t), "%s%d" % (b, t), "%s%d" % (sm, t)
            i = node("g", [lambda e, sn=sn, dn=dn, name=name: e.remote_dma(T[dn][:], T[sn][:], T.sem[name], T.sem.ls, pid, rid, mask)],
                     1.0, [A(sn)], [], (), "r", len(es))
            node(None, [], 0.0, [], [A(dn)], (), "a", (name, n_in), 2.5 if a == "qw" else 1.5, (i,))

    def update(t, c):
        ts(T.hf[:], T.hh[:], 16.0, OP.add, [A("hh")], [A("hf")], n=256)
        for b in range(2):
            mms([(T.p2[:, 128 * b:128 * b + 128], T.iv[:, 256 * par + 128 * b:256 * par + 128 * b + 128], T.hf[:, 128 * par:128 * par + 128],
                  par == 0, par == 1) for par in range(2)], 512, [A("iv"), A("hf")], [2])
        for H in range(2):
            kt, sc, wn = T["kt%d" % H], T["sc%d" % H], T["wn%d" % H]
            tt(wn[:], sc[:].indirect(T.cl[:]), kt[:], OP.is_equal, [A("kt%d" % H), A("cl"), A("sc%d" % H)], [A("wn%d" % H)], cost=0.25)
            mms([(T.p2[:, 256 + 128 * H:384 + 128 * H], wn[:], T.idn[:], True, True)], 128, [A("wn%d" % H), A("idn")], [2])
        E, M, S = A("ef%d" % c), A("mm%d" % c), A("sgn%d" % c)
        for b in range(2):
            d = T.de[:, 128 * b:128 * b + 128]
            e = T.ef[:, c + 4 * b::8]
            rg = ("de", b, b + 1)
            tt(d, T.p2[:, 128 * b:128 * b + 128], e, OP.subtract, [E], [rg], [2], n=128)
            tt(d, T.p2[:, 256 + b:512:2], d, OP.mult, [rg], [rg], [2], n=128)
            tt(e, e, d, OP.add, [E, rg], [("ef%d" % c, b, b + 1)], n=256)
        tt(T.tm[:], T.p2[:, 256:512], T.sgn[:, c::4], OP.mult, [S], [A("tm")], [2], n=256)
        tt(T.mm[:, c::4], T.mm[:, c::4], T.tm[:], OP.add, [M, A("tm")], [M], n=512)

    def out_lines(c):
        act(T.ylb[:, c::4], T.ef[:, c::4], AF.Copy, [A("ef%d" % c)], [A("yl%d" % c)], n=256, bias=-16.0)

    early_lists(0)
    prep_x(0)
    prep_s(0)
    for c in range(1, 4):
        early_lists(c)
    win = T.xw[:, XC:XW]
    WX = ("xw", XC, XW)
    for t in range(RO):
        c = t % 4
        first = t == 0
        gather_even(0)
        gather_even(1)
        gather_d(0)
        gather_d(1)
        hashes(0, 0, T.p0, 0, 0)
        hashes(1, 0, T.p1, 64, 1)
        hop(0, 64, T.p0[:, 0:64], 0, first)
        hop(64, 128, T.p1[:, 64:128], 1, first)
        scan(0)
        odd_min(0)
        hashes(0, 1, T.p1, 0, 1)
        scan(1)
        odd_min(1)
        hashes(1, 1, T.p2, 0, 2)
        hop(128, 192, T.p1[:, 0:64], 1, first)
        hop(192, 256, T.p2[:, 0:64], 2, first)
        for H, par in ((0, 0), (1, 0), (0, 1), (1, 1)):
            look(H, par)
        over(0)
        gate(0)
        over(1)
        gate(1)
        for H in range(2):
            score(H, 0, c)
            score(H, 1, c)
            keys(H)
        kl = T.p4[:, 0:16]
        mms([(T.p5[:, 0:16], T.idn[:], T.icn[:], True, False)], 64, [A("idn"), A("icn")], [5])
        ts(T.kn[:], kl, -1.0, OP.mult, [], [A("kn")], [4])
        ts(T.nf[:], kl, 0.75, OP.is_lt, [], [A("nf")], [4])
        ts(T.li[:], T.kn[:], 15, OP.bitwise_and, [A("kn")], [A("li")])
        tt(T.lj[:], T.li[:], T.i16[:], OP.add, [A("li"), A("i16")], [A("lj")])
        cp(T.l16[:], T.lj[:], [A("lj")], [A("l16")])
        qw, qn = T["qw%d" % t], "qw%d" % t
        cp(qw[:], T.qq[:].indirect(T.l16[:]), [A("qe"), A("qo"), A("l16")], [A(qn)], cost=0.05 + 256 * GAT)
        mms([(T.p1[:, 0:16], T.wu[:, 15 - r:143 - r], qw[:, r::16], r == 0, r == 15) for r in range(16)], 64, [A("wu"), A(qn)], [1])
        scn(T.nfs[:, 1:17], T.nf[:], T.z16[:], 0.0, OP.add, OP.max, [A("nf"), A("z16")], [A("nfs")], 16)
        tt(T.nfi[:], T.nf[:], T.icr[:], OP.mult, [A("nf"), A("icr")], [A("nfi")])
        mms([(T.p5[:, 0:16], T.am[:], T.nf[:], False, False), (T.p5[:, 0:16], T.nbl[:], T.nfs[:, 0:16], False, False),
             (T.p5[:, 0:16], T.idn[:], T.nfi[:], False, True)], 64, [A("am"), A("nf"), A("nbl"), A("nfs"), A("idn"), A("nfi")], [5])
        ts(T.ofi[:], T.p5[:, 0:16], 32.0, OP.mult, [], [A("ofi")], [5])
        cp(T.uwi[:], T.p1[:, 0:16], [], [A("uwi")], [1])
        ts(T.uwa[:], T.uwi[:], 31, OP.bitwise_and, [A("uwi")], [A("uwa")])
        tt(T.tgi[:], T.uwa[:], T.ofi[:], OP.add, [A("uwa"), A("ofi")], [A("tgi")])
        cp(T["tg%d" % t][:], T.tgi[:], [A("tgi")], [A("tg%d" % t)])
        send(t)
        if t == 3:
            update(t, c)
        if t < RO - 1:
            if t < 3:
                prep_x(t + 1)
                prep_s(t + 1)
            else:
                prep_x(0)
                prep_s(0)
            mms([(T.p5[:, 32:48], T.one[:], T.nf[:], True, True)], 64, [A("one"), A("nf")], [5])
            node("v", [lambda e: e.tensor_reduce(T.kc[:], T.p5[:, 32:48], AxisListType.X, OP.add)], cy(16), [], [A("kc")], [5])
            ts(T.kci[:], T.kc[:], -1.0, OP.mult, [A("kc")], [A("kci")])
            ts(T.kcj[:], T.kci[:], 31, OP.bitwise_and, [A("kci")], [A("kcj")])
            cp(T.kap[:], T.kcj[:], [A("kcj")], [A("kap")])
            ts(T.ek[:], T.ei[:], T.kap[:], OP.add, [A("ei"), A("kap")], [A("ek")], n=256)
        if t != 3:
            update(t, c)
        if t > 0:
            out_lines(c)
        lt = T["lt%d" % t]
        L = A("lt%d" % t)
        tt(T.av[:], win.indirect(lt[:]), T["lq%d" % t][:], OP.add, [WX, L, A("lq%d" % t)], [A("av")], cost=0.05 + 256 * GAT)
        ts(T.ai[:], T.av[:], 0.5, OP.mult, [A("av")], [A("ai")], (), -0.25, OP.add, n=256)
        cp(win.indirect(lt[:]), T.ai[:], [A("ai"), L], [WX], cost=0.05 + 256 * SCA)
    dma("y", T.ym[:], T.mm[:], MM4, [], 262144)
    dma("s", T.yl[:], T.ylb[:], [A("yl%d" % c) for c in range(4)], [], 524288)
    dma("y", T.yx[:, 0:2048], T.xw[:, XC:XC + 2048], [WX], [], 1048576)
    dma("s", T.yx[:, 2048:4096], T.xw[:, XC + 2048:XC + 4096], [WX], [], 1048576)

    n = len(nodes)
    before = [[] for _ in range(n)]
    after = [[] for _ in range(n)]
    for i, d in enumerate(nodes):
        for j in d["deps"] | d["order"]:
            f = nodes[j]
            lag = f["late"] + ((0.03 if f["q"] == d["q"] else 0.1) if j in d["deps"] else 0.0)
            before[i].append((j, lag))
            after[j].append((i, lag))

    def arrange(pre, post, prio):
        left = [len(x) for x in pre]
        end = [0.0] * n
        free = {q: 0.0 for q in eng}
        ready = {q: [] for q in eng}
        out, todo = [], [i for i in range(n) if not pre[i]]
        first = True
        while True:
            while todo:
                i = todo.pop()
                rel = [i] if first and not pre[i] else []
                if not rel:
                    for j, _ in post[i]:
                        left[j] -= 1
                        if left[j] == 0:
                            rel.append(j)
                for j in rel:
                    r = max([end[k] + lag for k, lag in pre[j]] + [0.0])
                    if nodes[j]["q"] is None:
                        end[j] = r
                        out.append(j)
                        todo.append(j)
                    else:
                        ready[nodes[j]["q"]].append((r, j))
            first = False
            best = None
            for q in eng:
                if ready[q]:
                    s0 = min(max(free[q], r) for r, _ in ready[q])
                    if best is None or s0 < best[0]:
                        best = (s0, q)
            if best is None:
                return out, end
            s0, q = best
            pick = max((x for x in ready[q] if max(free[q], x[0]) <= s0 + 0.06), key=lambda x: (prio[x[1]], -x[1]))
            ready[q].remove(pick)
            i = pick[1]
            free[q] = end[i] = max(free[q], pick[0]) + nodes[i]["cost"]
            out.append(i)
            todo.append(i)
    prio = [0.0] * n
    for i in range(n - 1, -1, -1):
        prio[i] = nodes[i]["cost"] + max([prio[j] + lag for j, lag in after[i]] + [0.0])
    best = None
    for _ in range(PASSES):
        out, end = arrange(before, after, prio)
        if best is None or max(end) < best[0]:
            best = (max(end), out, end)
        _, prio = arrange(after, before, end)
    orders, fin = best[1], best[2]

    cnt = {q: 0 for q in eng}
    known = {q: {} for q in eng}
    stamp, snap = {}, {}
    nloc = 0
    for i in orders:
        d = nodes[i]
        q = d["q"]
        if q is None:
            stamp[i] = (d["key"][0], 1, d["key"][1])
            snap[i] = {}
            continue
        kq = known[q]
        latest = {}
        for j in d["deps"]:
            s, k, v = stamp[j]
            if s not in latest or latest[s][0] < k:
                latest[s] = (k, v, j)
        for s in sorted(latest, key=lambda s: -fin[latest[s][2]]):
            k, v, j = latest[s]
            if kq.get(s, 0) >= k:
                continue
            eng[q].wait_ge(T.sem[s], v)
            kq[s] = k
            for s2, k2 in snap[j].items():
                if k2 > kq.get(s2, 0):
                    kq[s2] = k2
        snap[i] = dict(kq)
        if d["kind"] == "d":
            d["calls"][0](eng[q]).then_inc(T.sem[d["key"]], 16)
            stamp[i] = (d["key"], 1, 16)
        elif d["kind"] == "r":
            d["calls"][0](eng[q])
            nloc += d["key"]
            stamp[i] = ("ls", nloc, nloc)
        else:
            for f in d["calls"]:
                f(eng[q]).then_inc(T.sem[semname[q]], 1)
                cnt[q] += 1
            stamp[i] = (semname[q], cnt[q], cnt[q])
    for q in ("v", "s", "p", "g"):
        g.wait_ge(T.sem[semname[q]], cnt[q])
    for j in range(ndma[0]):
        g.wait_ge(T.sem["dm%d" % j], 16)
    g.wait_ge(T.sem.ls, nloc)
